import numpy as np
import ml_dtypes


def mxq(x, axis, fmt="e4m3"):
    dtype, down = {"e4m3": (ml_dtypes.float8_e4m3fn, 7), "e5m2": (ml_dtypes.float8_e5m2, 14)}[fmt]
    v = np.moveaxis(np.asarray(x, np.float32).astype(ml_dtypes.bfloat16).astype(np.float64), axis, -1)
    blocks = v.reshape(v.shape[:-1] + (-1, 32))
    amax = np.abs(blocks).max(-1, keepdims=True)
    byte = np.maximum(np.where(amax > 0, np.frexp(amax)[1] - 1 + 127, 0) - down, 1)
    scale = np.exp2(byte - 127.0)
    codes = (blocks / scale).astype(np.float32).astype(dtype).astype(np.float64)
    return np.moveaxis((codes * scale).reshape(v.shape), -1, axis)


WIDE = False


def mx_kscale(k):
    if not WIDE:
        return np.ones(k)
    levels = np.array([10, -10, 5, -5, 0])
    if k % 512:
        return np.exp2(np.random.permutation(np.resize(levels, k // 32))).repeat(32)
    a = np.empty((k // 512, 16))
    for p in range(k // 512):
        a[p, :8] = np.random.permutation(np.resize(levels, 8))
        for g in range(8):
            far = levels[np.abs(levels - a[p, g]) >= 10]
            a[p, g + 8] = far[np.random.randint(len(far))]
    return np.exp2(a.ravel()).repeat(32)


def f64(x):
    return np.asarray(x).astype(np.float64)


def striped(idx):
    return np.tile(idx.reshape(-1, 16).T, (8, 1)).astype(np.uint16)


def unstriped(offs):
    return offs[:16].T.reshape(-1).astype(np.int64)


E2M1 = np.array([0.0, 0.5, 1.0, 1.5, 2.0, 3.0, 4.0, 6.0, -0.0, -0.5, -1.0, -1.5, -2.0, -3.0, -4.0, -6.0])


def pack_weight(w, fmt):
    k, n = w.shape
    w = f64(np.asarray(w, np.float32).astype(ml_dtypes.bfloat16)).reshape(k // 32, 32, n)
    amax = np.abs(w).max(1)
    if fmt == "e4m3":
        byte = np.frexp(amax)[1] - 1 + 127 - 7
    else:
        mant, ex = np.frexp(amax / 6.0)
        byte = np.where(mant > 0.5, ex, ex - 1) + 127
    byte = np.clip(np.where(amax > 0, byte, 1), 1, 254)
    scaled = (w * np.exp2(127.0 - byte)[:, None, :]).reshape(k, n).astype(np.float32)
    by_word = np.ascontiguousarray(scaled.reshape(k // 512, 128, 4, n).transpose(0, 1, 3, 2))
    if fmt == "e4m3":
        words = by_word.astype(ml_dtypes.float8_e4m3fn).view(np.uint8)
    else:
        c = by_word.astype(ml_dtypes.float4_e2m1fn).view(np.uint8) & 0xF
        words = (c[..., 0::2] | (c[..., 1::2] << 4)).reshape(k // 512, 128, 2 * n)
    return np.ascontiguousarray(words), np.ascontiguousarray(byte.astype(np.uint8).reshape(k // 512, 16, n))


def unpack_weight(words, scales, fmt):
    g, _, n = scales.shape
    words = np.ascontiguousarray(words).reshape(g, 128, n, -1)
    if fmt == "e4m3":
        vals = words.view(ml_dtypes.float8_e4m3fn).astype(np.float64)
    else:
        nib = np.empty((g, 128, n, 4), np.uint8)
        nib[..., 0::2] = words & 0xF
        nib[..., 1::2] = words >> 4
        vals = E2M1[nib]
    vals = vals * np.repeat(np.exp2(scales.astype(np.float64) - 127.0), 8, axis=1)[..., None]
    return vals.transpose(0, 1, 3, 2).reshape(g * 512, n)


def relu2(v):
    return np.maximum(v, 0.0) ** 2


K, T, E, C, H, N = 512, 512, 8, 256, 512, 512


def by_expert(wq, xq):
    return np.concatenate([wq[e].T @ xq[:, e * C:(e + 1) * C] for e in range(E)], axis=1)


def setup_inputs():
    n = np.random.standard_normal
    s = mx_kscale(K)
    u = mx_kscale(H)
    slot_token = np.concatenate([np.random.permutation(T)[:C] for e in range(E)])
    partner = np.concatenate([np.random.permutation(T) for _ in range(-(-E * C // T))])[:E * C]
    x = pack_weight(n((K, T)) * s[:, None], "e4m3")
    w1 = [pack_weight(m, "e4m3") for m in n((E, K, H)) / np.sqrt(K) / s[None, :, None] * u]
    wp = [pack_weight(m, "e2m1") for m in n((E, K, H)) / np.sqrt(K) / s[None, :, None] * u]
    w2 = [pack_weight(m, "e4m3") for m in n((E, H, N)) / np.sqrt(H) / u[None, :, None] ** 2]
    return {
        "x_words": x[0],
        "x_scales": x[1],
        "w1_words": np.stack([m[0] for m in w1]),
        "w1_scales": np.stack([m[1] for m in w1]),
        "wp_words": np.stack([m[0] for m in wp]),
        "wp_scales": np.stack([m[1] for m in wp]),
        "w2_words": np.stack([m[0] for m in w2]),
        "w2_scales": np.stack([m[1] for m in w2]),
        "offs": striped(slot_token),
        "offs2": striped(partner),
    }


def reference(x_words, x_scales, w1_words, w1_scales, wp_words, wp_scales, w2_words, w2_scales, offs, offs2):
    w1 = np.stack([unpack_weight(w1_words[e], w1_scales[e], "e4m3") for e in range(E)])
    wp = np.stack([unpack_weight(wp_words[e], wp_scales[e], "e2m1") for e in range(E)])
    w2 = np.stack([unpack_weight(w2_words[e], w2_scales[e], "e4m3") for e in range(E)])
    idx, idx2 = unstriped(offs), unstriped(offs2)
    x = unpack_weight(x_words, x_scales, "e4m3")
    h = relu2(by_expert(w1, x[:, idx]) + by_expert(wp, x[:, idx2]))
    y = by_expert(w2, mxq(h, 0, "e4m3"))
    out = y
    return out

@@ -1,0 +1,188 @@
+from contextlib import ExitStack
+
+import concourse.mybir as mybir
+from concourse.masks import make_identity
+
+K, T, E, C, H, N = 512, 512, 8, 256, 512, 512
+FLOPS = 2 * E * C * (2 * K * H + H * N)
+
+F32 = mybir.dt.float32
+BF16 = mybir.dt.bfloat16
+I32 = mybir.dt.int32
+U32 = mybir.dt.uint32
+U16 = mybir.dt.uint16
+U8 = mybir.dt.uint8
+FP8X4 = mybir.dt.float8_e4m3fn_x4
+FP4X4 = mybir.dt.float4_e2m1fn_x4
+ACT = mybir.ActivationFunctionType
+ALU = mybir.AluOpType
+
+P = 128
+PACK = 4
+HALVES = C // P
+LIST_COLS = C // 16
+W1_ROW = 4
+W2_ROW = 8
+RING = 3
+LAG = 2
+VEC_RELU = {(7, 0), (7, 1)}
+VEC_OUT = {(e, 0) for e in range(E)}
+
+
+def tile_moe_duo_s_relu2_kernel(
+    tc, x_words, x_scales, w1_words, w1_scales, wp_words, wp_scales, w2_words, w2_scales, offs, offs2, out
+):
+    nc = tc.nc
+    with ExitStack() as ctx:
+        held = ctx.enter_context(tc.tile_pool(name="held", bufs=1))
+        ring = ctx.enter_context(tc.tile_pool(name="ring", bufs=1))
+        psum = ctx.enter_context(tc.psum_pool(name="psum", bufs=1))
+
+        tok_list = held.tile([P, E * LIST_COLS], U16, name="tok_list")
+        par_list = held.tile([P, E * LIST_COLS], U16, name="par_list")
+        x_w = held.tile([P, T], U32, name="x_w", align_bytes=64)
+        x_s = held.tile([P, T], U8, name="x_s", align_bytes=64)
+        s1 = held.tile([P, E * H], U8, name="s1", align_bytes=64)
+        s2 = held.tile([P, E * N], U8, name="s2", align_bytes=64)
+        ident = held.tile([P, P], F32, name="ident", align_bytes=64)
+        w1 = [held.tile([P, H], U32, name=f"w1_{e}", align_bytes=64) for e in range(E)]
+        wp = [held.tile([P, 2 * H], U8, name=f"wp_{e}", align_bytes=64) for e in range(E)]
+        w2 = [held.tile([P, N], U32, name=f"w2_{e}", align_bytes=64) for e in range(E)]
+
+        nc.vector.memset(x_s[:].bitcast(I32), 0)
+        nc.vector.memset(s1[:].bitcast(I32), 0)
+        nc.vector.memset(s2[:].bitcast(I32), 0)
+        make_identity(nc, ident[:])
+
+        def load_words(tile, words):
+            nc.sync.dma_start(tile[:].bitcast(I32), words.rearrange("p n d -> p (n d)").bitcast(I32))
+
+        def load_scales(tile, row, scales):
+            rows = scales.rearrange("e s b n -> b (e s) n")
+            for q in range(4):
+                nc.sync.dma_start(
+                    tile[32 * q + row : 32 * q + row + 4, :].bitcast(I32).rearrange("r (e n) -> r e n", e=E),
+                    rows[4 * q : 4 * q + 4].bitcast(I32),
+                )
+
+        def load_first(e):
+            load_words(w1[e], w1_words[e, 0])
+            nc.sync.dma_start(wp[e][:].bitcast(I32), wp_words[e, 0].bitcast(I32))
+
+        nc.sync.dma_start(tok_list[:], offs)
+        for q in range(4):
+            nc.sync.dma_start(
+                x_s[32 * q : 32 * q + 4, :].bitcast(I32), x_scales[0, 4 * q : 4 * q + 4, :].bitcast(I32)
+            )
+        load_words(x_w, x_words[0])
+        nc.sync.dma_start(par_list[:], offs2)
+        load_words(w1[0], w1_words[0, 0])
+        load_scales(s1, W1_ROW, w1_scales)
+        load_scales(s1, 0, wp_scales)
+        nc.sync.dma_start(wp[0][:].bitcast(I32), wp_words[0, 0].bitcast(I32))
+        load_first(1)
+        load_scales(s2, W2_ROW, w2_scales)
+        load_words(w2[0], w2_words[0, 0])
+        for e in range(2, E):
+            load_first(e)
+            load_words(w2[e - 1], w2_words[e - 1, 0])
+        load_words(w2[E - 1], w2_words[E - 1, 0])
+
+        pre = [psum.tile([P, H], F32, name=f"pre{i}") for i in range(2)]
+        turned = [psum.tile([P, PACK, P], F32, name=f"turned{i}") for i in range(2)]
+        res = [psum.tile([P, 2, C], F32, name=f"res{i}") for i in range(4)]
+
+        words, sbytes, relu, hidden, codes, cscales = {}, {}, {}, {}, {}, {}
+
+        def gather(e):
+            cols = slice(e * LIST_COLS, (e + 1) * LIST_COLS)
+            words[e] = ring.tile([P, 2 * C], U32, name=f"words{e}", tag=f"wide{e % RING}", align_bytes=64)
+            sbytes[e] = ring.tile([P, 2 * C], U8, name=f"bytes{e}", tag=f"relu{e % RING}", align_bytes=64)
+            nc.vector.tensor_copy(sbytes[e][:, 0:C], x_s[:].indirect(tok_list[:, cols]))
+            nc.vector.tensor_copy(words[e][:, 0:C], x_w[:].indirect(tok_list[:, cols]))
+            nc.vector.tensor_copy(sbytes[e][:, C : 2 * C], x_s[:].indirect(par_list[:, cols]))
+            nc.vector.tensor_copy(words[e][:, C : 2 * C], x_w[:].indirect(par_list[:, cols]))
+
+        def first_layer(e, a):
+            tok = slice(a * P, (a + 1) * P)
+            par = slice(C + a * P, C + (a + 1) * P)
+            cols = slice(e * H, (e + 1) * H)
+            nc.tensor.matmul_mx(
+                out=pre[a][:], lhsT=words[e][:, tok].bitcast(FP8X4), lhsT_scale=sbytes[e][:, tok],
+                rhs=w1[e][:].bitcast(FP8X4), rhs_scale=s1[W1_ROW:P, cols], start=True, stop=False,
+            )
+            nc.tensor.matmul_mx(
+                out=pre[a][:], lhsT=words[e][:, par].bitcast(FP8X4), lhsT_scale=sbytes[e][:, par],
+                rhs=wp[e][:].bitcast(FP4X4), rhs_scale=s1[:, cols], start=False, stop=True,
+            )
+
+        def rectify(e, a):
+            tag = f"relu{e % RING}" if a == HALVES - 1 else f"relu_first{e % 2}"
+            relu[e, a] = ring.tile([P, PACK, P], F32, name=f"relu{e}_{a}", tag=tag, align_bytes=64)
+            src = pre[a][:].rearrange("s (p t) -> s t p", t=PACK)
+            if (e, a) in VEC_RELU:
+                nc.vector.tensor_scalar_max(relu[e, a][:], src, 0.0)
+            else:
+                nc.scalar.activation(relu[e, a][:], src, ACT.Relu)
+
+        def turn(e, a):
+            bank = turned[a]
+            for t in range(PACK):
+                nc.tensor.transpose(bank[:, t, :], relu[e, a][:, t, :], ident[:])
+
+        def square(e, a):
+            if a == 0:
+                hidden[e] = ring.tile([P, C, PACK], BF16, name=f"hidden{e}", tag=f"wide{e % RING}", align_bytes=64)
+            bank = turned[a]
+            nc.scalar.activation(
+                hidden[e][:, a * P : (a + 1) * P, :], bank[:].rearrange("p t s -> p s t"), ACT.Square
+            )
+
+        def quantize(e):
+            codes[e] = ring.tile([P, C], U32, name=f"codes{e}", tag=f"codes{e % 2}", align_bytes=64)
+            cscales[e] = ring.tile([P, C], U8, name=f"cscales{e}", tag=f"cscales{e % 2}", align_bytes=64)
+            nc.vector.quantize_mx(
+                out=codes[e][:].bitcast(FP8X4), scales=cscales[e][:],
+                in_=hidden[e][:].rearrange("p s t -> p (s t)"),
+            )
+
+        def second_layer(e, a):
+            bank = res[(2 * e + a) % 4]
+            for j in range(2):
+                n0 = (2 * a + j) * P
+                nc.tensor.matmul_mx(
+                    out=bank[:, j, :], lhsT=w2[e][:, n0 : n0 + P].bitcast(FP8X4),
+                    lhsT_scale=s2[W2_ROW:P, e * N + n0 : e * N + n0 + P],
+                    rhs=codes[e][:].bitcast(FP8X4), rhs_scale=cscales[e][:], start=True, stop=True,
+                )
+
+        def emit(e, a):
+            bank = res[(2 * e + a) % 4]
+            staged = ring.tile([P, 2, C], F32, name=f"staged{e}_{a}", tag="staged", bufs=6, align_bytes=64)
+            if (e, a) in VEC_OUT:
+                nc.vector.tensor_copy(staged[:], bank[:])
+            else:
+                nc.scalar.copy(staged[:], bank[:])
+            rows = out[2 * a * P : 2 * (a + 1) * P, e * C : (e + 1) * C]
+            nc.sync.dma_start(rows.rearrange("(j p) c -> p j c", p=P), staged[:])
+
+        for e in range(RING):
+            gather(e)
+        for step in range(E + LAG):
+            e, late = step, step - LAG
+            if e < E:
+                for a in range(HALVES):
+                    first_layer(e, a)
+                    rectify(e, a)
+                for a in range(HALVES):
+                    turn(e, a)
+            if late >= 0:
+                for a in range(2):
+                    second_layer(late, a)
+                    emit(late, a)
+            if e < E:
+                for a in range(HALVES):
+                    square(e, a)
+                quantize(e)
+                if e + RING < E:
+                    gather(e + RING)

@@ -25,8 +25,11 @@ W1_ROW = 4
 W2_ROW = 8
 RING = 3
 LAG = 2
-VEC_RELU = {(7, 0), (7, 1)}
-VEC_OUT = {(e, 0) for e in range(E)}
+EARLY = 2
+TIE_HALF = 1
+FINE = 2
+VEC_RELU = {(e, a) for e in range(E) for a in range(HALVES) if HALVES * e + a >= 11}
+VEC_OUT = {(e, 0) for e in range(4, E)}
 
 
 def tile_moe_duo_s_relu2_kernel(
@@ -42,88 +45,98 @@ def tile_moe_duo_s_relu2_kernel(
         par_list = held.tile([P, E * LIST_COLS], U16, name="par_list")
         x_w = held.tile([P, T], U32, name="x_w", align_bytes=64)
         x_s = held.tile([P, T], U8, name="x_s", align_bytes=64)
-        s1 = held.tile([P, E * H], U8, name="s1", align_bytes=64)
-        s2 = held.tile([P, E * N], U8, name="s2", align_bytes=64)
+        s_early = held.tile([P, EARLY * H], U8, name="s_early", align_bytes=64)
+        s_main = held.tile([P, E * H], U8, name="s_main", align_bytes=64)
         ident = held.tile([P, P], F32, name="ident", align_bytes=64)
         w1 = [held.tile([P, H], U32, name=f"w1_{e}", align_bytes=64) for e in range(E)]
         wp = [held.tile([P, 2 * H], U8, name=f"wp_{e}", align_bytes=64) for e in range(E)]
         w2 = [held.tile([P, N], U32, name=f"w2_{e}", align_bytes=64) for e in range(E)]
 
-        nc.vector.memset(x_s[:].bitcast(I32), 0)
-        nc.vector.memset(s1[:].bitcast(I32), 0)
-        nc.vector.memset(s2[:].bitcast(I32), 0)
+        nc.gpsimd.memset(x_s[:].bitcast(I32), 0)
+        nc.gpsimd.memset(s_early[:].bitcast(I32), 0)
+        nc.gpsimd.dma_start(wp[0][:].bitcast(I32), wp_words[0, 0].bitcast(I32))
         make_identity(nc, ident[:])
+        nc.vector.memset(s_main[:].bitcast(I32), 0)
 
         def load_words(tile, words):
             nc.sync.dma_start(tile[:].bitcast(I32), words.rearrange("p n d -> p (n d)").bitcast(I32))
 
-        def load_scales(tile, row, scales):
+        def load_scales(tile, row, scales, first, last):
             rows = scales.rearrange("e s b n -> b (e s) n")
             for q in range(4):
+                dst = tile[32 * q + row : 32 * q + row + 4, first * H : last * H].bitcast(I32)
                 nc.sync.dma_start(
-                    tile[32 * q + row : 32 * q + row + 4, :].bitcast(I32).rearrange("r (e n) -> r e n", e=E),
-                    rows[4 * q : 4 * q + 4].bitcast(I32),
+                    dst.rearrange("r (e n) -> r e n", e=last - first),
+                    rows[4 * q : 4 * q + 4, first:last, :].bitcast(I32),
                 )
 
         def load_first(e):
             load_words(w1[e], w1_words[e, 0])
             nc.sync.dma_start(wp[e][:].bitcast(I32), wp_words[e, 0].bitcast(I32))
 
-        nc.sync.dma_start(tok_list[:], offs)
         for q in range(4):
             nc.sync.dma_start(
                 x_s[32 * q : 32 * q + 4, :].bitcast(I32), x_scales[0, 4 * q : 4 * q + 4, :].bitcast(I32)
             )
-        load_words(x_w, x_words[0])
+        nc.sync.dma_start(tok_list[:], offs)
         nc.sync.dma_start(par_list[:], offs2)
+        load_words(x_w, x_words[0])
         load_words(w1[0], w1_words[0, 0])
-        load_scales(s1, W1_ROW, w1_scales)
-        load_scales(s1, 0, wp_scales)
-        nc.sync.dma_start(wp[0][:].bitcast(I32), wp_words[0, 0].bitcast(I32))
+        load_scales(s_early, W1_ROW, w1_scales, 0, EARLY)
+        load_scales(s_early, 0, wp_scales, 0, EARLY)
         load_first(1)
-        load_scales(s2, W2_ROW, w2_scales)
+        load_scales(s_main, W1_ROW, w1_scales, EARLY, E)
+        load_scales(s_main, 0, wp_scales, EARLY, E)
+        load_first(2)
+        load_scales(s_main, W2_ROW, w2_scales, 0, E)
         load_words(w2[0], w2_words[0, 0])
-        for e in range(2, E):
+        load_words(w2[1], w2_words[1, 0])
+        for e in range(3, E):
             load_first(e)
             load_words(w2[e - 1], w2_words[e - 1, 0])
         load_words(w2[E - 1], w2_words[E - 1, 0])
 
-        pre = [psum.tile([P, H], F32, name=f"pre{i}") for i in range(2)]
+        pre = [psum.tile([P, H], F32, name=f"pre{i}") for i in range(3)]
         turned = [psum.tile([P, PACK, P], F32, name=f"turned{i}") for i in range(2)]
-        res = [psum.tile([P, 2, C], F32, name=f"res{i}") for i in range(4)]
+        res = [psum.tile([P, N], F32, name=f"res{i}") for i in range(3)]
 
         words, sbytes, relu, hidden, codes, cscales = {}, {}, {}, {}, {}, {}
 
-        def gather(e):
+        def gather_bytes(e, tag):
+            cols = slice(e * LIST_COLS, (e + 1) * LIST_COLS)
+            sbytes[e] = ring.tile([P, 2 * C], U8, name=f"bytes{e}", tag=tag, align_bytes=64)
+            nc.vector.tensor_copy(sbytes[e][:, 0:C], x_s[:].indirect(tok_list[:, cols]))
+            nc.vector.tensor_copy(sbytes[e][:, C : 2 * C], x_s[:].indirect(par_list[:, cols]))
+
+        def gather_words(e):
             cols = slice(e * LIST_COLS, (e + 1) * LIST_COLS)
             words[e] = ring.tile([P, 2 * C], U32, name=f"words{e}", tag=f"wide{e % RING}", align_bytes=64)
-            sbytes[e] = ring.tile([P, 2 * C], U8, name=f"bytes{e}", tag=f"relu{e % RING}", align_bytes=64)
-            nc.vector.tensor_copy(sbytes[e][:, 0:C], x_s[:].indirect(tok_list[:, cols]))
             nc.vector.tensor_copy(words[e][:, 0:C], x_w[:].indirect(tok_list[:, cols]))
-            nc.vector.tensor_copy(sbytes[e][:, C : 2 * C], x_s[:].indirect(par_list[:, cols]))
             nc.vector.tensor_copy(words[e][:, C : 2 * C], x_w[:].indirect(par_list[:, cols]))
 
         def first_layer(e, a):
             tok = slice(a * P, (a + 1) * P)
             par = slice(C + a * P, C + (a + 1) * P)
             cols = slice(e * H, (e + 1) * H)
+            s1 = s_early if e < EARLY else s_main
             nc.tensor.matmul_mx(
-                out=pre[a][:], lhsT=words[e][:, tok].bitcast(FP8X4), lhsT_scale=sbytes[e][:, tok],
+                out=pre[(HALVES * e + a) % 3][:], lhsT=words[e][:, tok].bitcast(FP8X4), lhsT_scale=sbytes[e][:, tok],
                 rhs=w1[e][:].bitcast(FP8X4), rhs_scale=s1[W1_ROW:P, cols], start=True, stop=False,
             )
             nc.tensor.matmul_mx(
-                out=pre[a][:], lhsT=words[e][:, par].bitcast(FP8X4), lhsT_scale=sbytes[e][:, par],
+                out=pre[(HALVES * e + a) % 3][:], lhsT=words[e][:, par].bitcast(FP8X4), lhsT_scale=sbytes[e][:, par],
                 rhs=wp[e][:].bitcast(FP4X4), rhs_scale=s1[:, cols], start=False, stop=True,
             )
 
         def rectify(e, a):
-            tag = f"relu{e % RING}" if a == HALVES - 1 else f"relu_first{e % 2}"
+            tag = f"half{HALVES * e + a}"
             relu[e, a] = ring.tile([P, PACK, P], F32, name=f"relu{e}_{a}", tag=tag, align_bytes=64)
-            src = pre[a][:].rearrange("s (p t) -> s t p", t=PACK)
+            src = pre[(HALVES * e + a) % 3][:].rearrange("s (g u t) -> s g t u", u=PACK, t=PACK)
+            dst = relu[e, a][:].rearrange("s t (g u) -> s g t u", u=PACK)
             if (e, a) in VEC_RELU:
-                nc.vector.tensor_scalar_max(relu[e, a][:], src, 0.0)
+                nc.vector.tensor_scalar_max(dst, src, 0.0)
             else:
-                nc.scalar.activation(relu[e, a][:], src, ACT.Relu)
+                nc.scalar.activation(dst, src, ACT.Relu)
 
         def turn(e, a):
             bank = turned[a]
@@ -138,36 +151,43 @@ def tile_moe_duo_s_relu2_kernel(
                 hidden[e][:, a * P : (a + 1) * P, :], bank[:].rearrange("p t s -> p s t"), ACT.Square
             )
 
-        def quantize(e):
-            codes[e] = ring.tile([P, C], U32, name=f"codes{e}", tag=f"codes{e % 2}", align_bytes=64)
-            cscales[e] = ring.tile([P, C], U8, name=f"cscales{e}", tag=f"cscales{e % 2}", align_bytes=64)
+        def quantize(e, first, last):
+            if first == 0:
+                codes[e] = ring.tile([P, C], U32, name=f"codes{e}", align_bytes=64)
+                cscales[e] = ring.tile([P, C], U8, name=f"cscales{e}", align_bytes=64)
             nc.vector.quantize_mx(
-                out=codes[e][:].bitcast(FP8X4), scales=cscales[e][:],
-                in_=hidden[e][:].rearrange("p s t -> p (s t)"),
+                out=codes[e][:, first:last].bitcast(FP8X4), scales=cscales[e][:, first:last],
+                in_=hidden[e][:, first:last, :].rearrange("p s t -> p (s t)"),
             )
 
         def second_layer(e, a):
-            bank = res[(2 * e + a) % 4]
-            for j in range(2):
-                n0 = (2 * a + j) * P
+            if e >= E - FINE:
+                blocks, slots = range(N // P), slice(a * P, (a + 1) * P)
+            else:
+                blocks, slots = range(2 * a, 2 * a + 2), slice(0, C)
+            width = slots.stop - slots.start
+            bank = res[(2 * e + a) % 3]
+            for j, block in enumerate(blocks):
+                n0 = block * P
                 nc.tensor.matmul_mx(
-                    out=bank[:, j, :], lhsT=w2[e][:, n0 : n0 + P].bitcast(FP8X4),
-                    lhsT_scale=s2[W2_ROW:P, e * N + n0 : e * N + n0 + P],
-                    rhs=codes[e][:].bitcast(FP8X4), rhs_scale=cscales[e][:], start=True, stop=True,
+                    out=bank[:, j * width : (j + 1) * width], lhsT=w2[e][:, n0 : n0 + P].bitcast(FP8X4),
+                    lhsT_scale=s_main[W2_ROW:P, e * N + n0 : e * N + n0 + P],
+                    rhs=codes[e][:, slots].bitcast(FP8X4), rhs_scale=cscales[e][:, slots], start=True, stop=True,
                 )
-
-        def emit(e, a):
-            bank = res[(2 * e + a) % 4]
-            staged = ring.tile([P, 2, C], F32, name=f"staged{e}_{a}", tag="staged", bufs=6, align_bytes=64)
+            staged = ring.tile([P, N], F32, name=f"staged{e}_{a}", align_bytes=64)
             if (e, a) in VEC_OUT:
                 nc.vector.tensor_copy(staged[:], bank[:])
             else:
                 nc.scalar.copy(staged[:], bank[:])
-            rows = out[2 * a * P : 2 * (a + 1) * P, e * C : (e + 1) * C]
-            nc.sync.dma_start(rows.rearrange("(j p) c -> p j c", p=P), staged[:])
+            rows = out[blocks.start * P : blocks.stop * P, e * C + slots.start : e * C + slots.stop]
+            nc.sync.dma_start(
+                rows.rearrange("(j p) c -> p j c", p=P), staged[:].rearrange("p (j c) -> p j c", c=width)
+            )
 
         for e in range(RING):
-            gather(e)
+            if e < EARLY:
+                gather_bytes(e, f"bytes{e}")
+            gather_words(e)
         for step in range(E + LAG):
             e, late = step, step - LAG
             if e < E:
@@ -176,13 +196,20 @@ def tile_moe_duo_s_relu2_kernel(
                     rectify(e, a)
                 for a in range(HALVES):
                     turn(e, a)
+                    half = HALVES * e + a
+                    if half == 0:
+                        gather_bytes(EARLY, "half0")
+                    if a == TIE_HALF and e + RING < E and half > 0:
+                        gather_bytes(e + RING, f"half{half}")
             if late >= 0:
                 for a in range(2):
                     second_layer(late, a)
-                    emit(late, a)
             if e < E:
                 for a in range(HALVES):
                     square(e, a)
-                quantize(e)
+                    if e >= E - FINE:
+                        quantize(e, a * P, (a + 1) * P)
+                if e < E - FINE:
+                    quantize(e, 0, C)
                 if e + RING < E:
-                    gather(e + RING)
+                    gather_words(e + RING)

@@ -27,8 +27,10 @@ RING = 3
 LAG = 2
 EARLY = 2
 TIE_HALF = 1
-FINE = 2
-VEC_RELU = {(e, a) for e in range(E) for a in range(HALVES) if HALVES * e + a >= 11}
+FINE = 0
+GROUPS_1 = [(0, 1), (1, 3), (3, 5), (5, 8)]
+GROUPS_2 = [(0, 2), (2, 5), (5, 8)]
+VEC_RELU = {(e, a) for e in range(E) for a in range(HALVES) if HALVES * e + a >= 12}
 VEC_OUT = {(e, 0) for e in range(4, E)}
 
 
@@ -45,34 +47,36 @@ def tile_moe_duo_s_relu2_kernel(
         par_list = held.tile([P, E * LIST_COLS], U16, name="par_list")
         x_w = held.tile([P, T], U32, name="x_w", align_bytes=64)
         x_s = held.tile([P, T], U8, name="x_s", align_bytes=64)
-        s_early = held.tile([P, EARLY * H], U8, name="s_early", align_bytes=64)
-        s_main = held.tile([P, E * H], U8, name="s_main", align_bytes=64)
+        s1 = held.tile([P, E * H], U8, name="s1", align_bytes=64)
+        s2 = held.tile([P, E * N], U8, name="s2", align_bytes=64)
         ident = held.tile([P, P], F32, name="ident", align_bytes=64)
-        w1 = [held.tile([P, H], U32, name=f"w1_{e}", align_bytes=64) for e in range(E)]
-        wp = [held.tile([P, 2 * H], U8, name=f"wp_{e}", align_bytes=64) for e in range(E)]
-        w2 = [held.tile([P, N], U32, name=f"w2_{e}", align_bytes=64) for e in range(E)]
+        w1, wp, w2 = {}, {}, {}
+
+        def load_group(queue, store, words, first, last, name, dtype):
+            row_words = words.shape[-1]
+            width = row_words if dtype == U32 else 4 * row_words
+            tile = held.tile([P, last - first, width], dtype, name=f"{name}_{first}", align_bytes=64)
+            queue.dma_start(tile[:].bitcast(I32), words[first:last].rearrange("e p n -> p e n"))
+            for e in range(first, last):
+                store[e] = tile[:, e - first, :]
+
+        w1_src = w1_words.rearrange("e s p n d -> e (s p) (n d)").bitcast(I32)
+        wp_src = wp_words.rearrange("e s p n -> e (s p) n").bitcast(I32)
+        w2_src = w2_words.rearrange("e s p n d -> e (s p) (n d)").bitcast(I32)
 
         nc.gpsimd.memset(x_s[:].bitcast(I32), 0)
-        nc.gpsimd.memset(s_early[:].bitcast(I32), 0)
-        nc.gpsimd.dma_start(wp[0][:].bitcast(I32), wp_words[0, 0].bitcast(I32))
+        load_group(nc.gpsimd, wp, wp_src, *GROUPS_1[0], "wp", U8)
         make_identity(nc, ident[:])
-        nc.vector.memset(s_main[:].bitcast(I32), 0)
+        nc.vector.memset(s1[:].bitcast(I32), 0)
+        nc.vector.memset(s2[:].bitcast(I32), 0)
 
-        def load_words(tile, words):
-            nc.sync.dma_start(tile[:].bitcast(I32), words.rearrange("p n d -> p (n d)").bitcast(I32))
-
-        def load_scales(tile, row, scales, first, last):
+        def load_scales(tile, row, scales):
             rows = scales.rearrange("e s b n -> b (e s) n")
             for q in range(4):
-                dst = tile[32 * q + row : 32 * q + row + 4, first * H : last * H].bitcast(I32)
+                dst = tile[32 * q + row : 32 * q + row + 4, :].bitcast(I32)
                 nc.sync.dma_start(
-                    dst.rearrange("r (e n) -> r e n", e=last - first),
-                    rows[4 * q : 4 * q + 4, first:last, :].bitcast(I32),
+                    dst.rearrange("r (e n) -> r e n", e=E), rows[4 * q : 4 * q + 4].bitcast(I32)
                 )
-
-        def load_first(e):
-            load_words(w1[e], w1_words[e, 0])
-            nc.sync.dma_start(wp[e][:].bitcast(I32), wp_words[e, 0].bitcast(I32))
 
         for q in range(4):
             nc.sync.dma_start(
@@ -80,21 +84,16 @@ def tile_moe_duo_s_relu2_kernel(
             )
         nc.sync.dma_start(tok_list[:], offs)
         nc.sync.dma_start(par_list[:], offs2)
-        load_words(x_w, x_words[0])
-        load_words(w1[0], w1_words[0, 0])
-        load_scales(s_early, W1_ROW, w1_scales, 0, EARLY)
-        load_scales(s_early, 0, wp_scales, 0, EARLY)
-        load_first(1)
-        load_scales(s_main, W1_ROW, w1_scales, EARLY, E)
-        load_scales(s_main, 0, wp_scales, EARLY, E)
-        load_first(2)
-        load_scales(s_main, W2_ROW, w2_scales, 0, E)
-        load_words(w2[0], w2_words[0, 0])
-        load_words(w2[1], w2_words[1, 0])
-        for e in range(3, E):
-            load_first(e)
-            load_words(w2[e - 1], w2_words[e - 1, 0])
-        load_words(w2[E - 1], w2_words[E - 1, 0])
+        nc.sync.dma_start(x_w[:].bitcast(I32), x_words[0].rearrange("p n d -> p (n d)").bitcast(I32))
+        load_group(nc.sync, w1, w1_src, *GROUPS_1[0], "w1", U32)
+        load_scales(s1, W1_ROW, w1_scales)
+        load_scales(s1, 0, wp_scales)
+        for g in range(1, len(GROUPS_1)):
+            load_group(nc.sync, w1, w1_src, *GROUPS_1[g], "w1", U32)
+            load_group(nc.sync, wp, wp_src, *GROUPS_1[g], "wp", U8)
+            if g == 1:
+                load_scales(s2, W2_ROW, w2_scales)
+            load_group(nc.sync, w2, w2_src, *GROUPS_2[g - 1], "w2", U32)
 
         pre = [psum.tile([P, H], F32, name=f"pre{i}") for i in range(3)]
         turned = [psum.tile([P, PACK, P], F32, name=f"turned{i}") for i in range(2)]
@@ -118,14 +117,13 @@ def tile_moe_duo_s_relu2_kernel(
             tok = slice(a * P, (a + 1) * P)
             par = slice(C + a * P, C + (a + 1) * P)
             cols = slice(e * H, (e + 1) * H)
-            s1 = s_early if e < EARLY else s_main
             nc.tensor.matmul_mx(
                 out=pre[(HALVES * e + a) % 3][:], lhsT=words[e][:, tok].bitcast(FP8X4), lhsT_scale=sbytes[e][:, tok],
-                rhs=w1[e][:].bitcast(FP8X4), rhs_scale=s1[W1_ROW:P, cols], start=True, stop=False,
+                rhs=w1[e].bitcast(FP8X4), rhs_scale=s1[W1_ROW:P, cols], start=True, stop=False,
             )
             nc.tensor.matmul_mx(
                 out=pre[(HALVES * e + a) % 3][:], lhsT=words[e][:, par].bitcast(FP8X4), lhsT_scale=sbytes[e][:, par],
-                rhs=wp[e][:].bitcast(FP4X4), rhs_scale=s1[:, cols], start=False, stop=True,
+                rhs=wp[e].bitcast(FP4X4), rhs_scale=s1[:, cols], start=False, stop=True,
             )
 
         def rectify(e, a):
@@ -171,7 +169,7 @@ def tile_moe_duo_s_relu2_kernel(
                 n0 = block * P
                 nc.tensor.matmul_mx(
                     out=bank[:, j * width : (j + 1) * width], lhsT=w2[e][:, n0 : n0 + P].bitcast(FP8X4),
-                    lhsT_scale=s_main[W2_ROW:P, e * N + n0 : e * N + n0 + P],
+                    lhsT_scale=s2[W2_ROW:P, e * N + n0 : e * N + n0 + P],
                     rhs=codes[e][:, slots].bitcast(FP8X4), rhs_scale=cscales[e][:, slots], start=True, stop=True,
                 )
             staged = ring.tile([P, N], F32, name=f"staged{e}_{a}", align_bytes=64)

@@ -23,15 +23,15 @@ HALVES = C // P
 LIST_COLS = C // 16
 W1_ROW = 4
 W2_ROW = 8
-RING = 3
-LAG = 2
+RING = 4
+LAG = 3
 EARLY = 2
 TIE_HALF = 1
 FINE = 0
 GROUPS_1 = [(0, 1), (1, 3), (3, 5), (5, 8)]
 GROUPS_2 = [(0, 2), (2, 5), (5, 8)]
 VEC_RELU = {(e, a) for e in range(E) for a in range(HALVES) if HALVES * e + a >= 12}
-VEC_OUT = {(e, 0) for e in range(4, E)}
+VEC_OUT = {(e, 0) for e in range(3, E)}
 
 
 def tile_moe_duo_s_relu2_kernel(
@@ -95,9 +95,8 @@ def tile_moe_duo_s_relu2_kernel(
                 load_scales(s2, W2_ROW, w2_scales)
             load_group(nc.sync, w2, w2_src, *GROUPS_2[g - 1], "w2", U32)
 
-        pre = [psum.tile([P, H], F32, name=f"pre{i}") for i in range(3)]
-        turned = [psum.tile([P, PACK, P], F32, name=f"turned{i}") for i in range(2)]
-        res = [psum.tile([P, N], F32, name=f"res{i}") for i in range(3)]
+        work = [[psum.tile([P, H], F32, name=f"work{i}_{a}") for a in range(HALVES)] for i in range(2)]
+        res = [psum.tile([P, N], F32, name=f"res{i}") for i in range(4)]
 
         words, sbytes, relu, hidden, codes, cscales = {}, {}, {}, {}, {}, {}
 
@@ -118,18 +117,18 @@ def tile_moe_duo_s_relu2_kernel(
             par = slice(C + a * P, C + (a + 1) * P)
             cols = slice(e * H, (e + 1) * H)
             nc.tensor.matmul_mx(
-                out=pre[(HALVES * e + a) % 3][:], lhsT=words[e][:, tok].bitcast(FP8X4), lhsT_scale=sbytes[e][:, tok],
+                out=work[e % 2][a][:], lhsT=words[e][:, tok].bitcast(FP8X4), lhsT_scale=sbytes[e][:, tok],
                 rhs=w1[e].bitcast(FP8X4), rhs_scale=s1[W1_ROW:P, cols], start=True, stop=False,
             )
             nc.tensor.matmul_mx(
-                out=pre[(HALVES * e + a) % 3][:], lhsT=words[e][:, par].bitcast(FP8X4), lhsT_scale=sbytes[e][:, par],
+                out=work[e % 2][a][:], lhsT=words[e][:, par].bitcast(FP8X4), lhsT_scale=sbytes[e][:, par],
                 rhs=wp[e].bitcast(FP4X4), rhs_scale=s1[:, cols], start=False, stop=True,
             )
 
         def rectify(e, a):
             tag = f"half{HALVES * e + a}"
             relu[e, a] = ring.tile([P, PACK, P], F32, name=f"relu{e}_{a}", tag=tag, align_bytes=64)
-            src = pre[(HALVES * e + a) % 3][:].rearrange("s (g u t) -> s g t u", u=PACK, t=PACK)
+            src = work[e % 2][a][:].rearrange("s (g u t) -> s g t u", u=PACK, t=PACK)
             dst = relu[e, a][:].rearrange("s t (g u) -> s g t u", u=PACK)
             if (e, a) in VEC_RELU:
                 nc.vector.tensor_scalar_max(dst, src, 0.0)
@@ -137,16 +136,16 @@ def tile_moe_duo_s_relu2_kernel(
                 nc.scalar.activation(dst, src, ACT.Relu)
 
         def turn(e, a):
-            bank = turned[a]
+            bank = work[e % 2][1 - a][:].rearrange("p (t s) -> p t s", t=PACK)
             for t in range(PACK):
                 nc.tensor.transpose(bank[:, t, :], relu[e, a][:, t, :], ident[:])
 
         def square(e, a):
             if a == 0:
                 hidden[e] = ring.tile([P, C, PACK], BF16, name=f"hidden{e}", tag=f"wide{e % RING}", align_bytes=64)
-            bank = turned[a]
+            bank = work[e % 2][1 - a][:].rearrange("p (t s) -> p t s", t=PACK)
             nc.scalar.activation(
-                hidden[e][:, a * P : (a + 1) * P, :], bank[:].rearrange("p t s -> p s t"), ACT.Square
+                hidden[e][:, a * P : (a + 1) * P, :], bank.rearrange("p t s -> p s t"), ACT.Square
             )
 
         def quantize(e, first, last):
@@ -164,7 +163,7 @@ def tile_moe_duo_s_relu2_kernel(
             else:
                 blocks, slots = range(2 * a, 2 * a + 2), slice(0, C)
             width = slots.stop - slots.start
-            bank = res[(2 * e + a) % 3]
+            bank = res[(2 * e + a) % 4]
             for j, block in enumerate(blocks):
                 n0 = block * P
                 nc.tensor.matmul_mx(
@@ -184,21 +183,18 @@ def tile_moe_duo_s_relu2_kernel(
 
         for e in range(RING):
             if e < EARLY:
-                gather_bytes(e, f"bytes{e}")
+                gather_bytes(e, f"bytes{e % EARLY}")
             gather_words(e)
         for step in range(E + LAG):
             e, late = step, step - LAG
             if e < E:
                 for a in range(HALVES):
                     first_layer(e, a)
+                    if a == HALVES - 1 and e + EARLY < E:
+                        gather_bytes(e + EARLY, f"bytes{e % EARLY}")
                     rectify(e, a)
                 for a in range(HALVES):
                     turn(e, a)
-                    half = HALVES * e + a
-                    if half == 0:
-                        gather_bytes(EARLY, "half0")
-                    if a == TIE_HALF and e + RING < E and half > 0:
-                        gather_bytes(e + RING, f"half{half}")
             if late >= 0:
                 for a in range(2):
                     second_layer(late, a)

@@ -21,17 +21,18 @@ P = 128
 PACK = 4
 HALVES = C // P
 LIST_COLS = C // 16
-W1_ROW = 4
-W2_ROW = 8
-RING = 4
-LAG = 3
-EARLY = 2
-TIE_HALF = 1
-FINE = 0
+PLANES = 4
+WORD_RING = 4
+BYTE_RING = 2
+FIRST_BANKS = 3
+TURN_BANKS = 2
+RESULT_BANKS = 3
 GROUPS_1 = [(0, 1), (1, 3), (3, 5), (5, 8)]
 GROUPS_2 = [(0, 2), (2, 5), (5, 8)]
-VEC_RELU = {(e, a) for e in range(E) for a in range(HALVES) if HALVES * e + a >= 12}
-VEC_OUT = {(e, 0) for e in range(3, E)}
+VEC_RELU_FROM = 13
+VEC_OUT_FROM = 3
+SQUARE_LAG = 1
+OUT_LAG = 2
 
 
 def tile_moe_duo_s_relu2_kernel(
@@ -47,8 +48,9 @@ def tile_moe_duo_s_relu2_kernel(
         par_list = held.tile([P, E * LIST_COLS], U16, name="par_list")
         x_w = held.tile([P, T], U32, name="x_w", align_bytes=64)
         x_s = held.tile([P, T], U8, name="x_s", align_bytes=64)
-        s1 = held.tile([P, E * H], U8, name="s1", align_bytes=64)
-        s2 = held.tile([P, E * N], U8, name="s2", align_bytes=64)
+        sp = held.tile([P, E * H], U8, name="sp", align_bytes=64)
+        s1 = held.tile([P, E // PLANES * H], U8, name="s1", align_bytes=64)
+        s2 = held.tile([P, E // PLANES * N], U8, name="s2", align_bytes=64)
         ident = held.tile([P, P], F32, name="ident", align_bytes=64)
         w1, wp, w2 = {}, {}, {}
 
@@ -68,142 +70,137 @@ def tile_moe_duo_s_relu2_kernel(
         load_group(nc.gpsimd, wp, wp_src, *GROUPS_1[0], "wp", U8)
         make_identity(nc, ident[:])
         nc.vector.memset(s1[:].bitcast(I32), 0)
+        nc.vector.memset(sp[:].bitcast(I32), 0)
         nc.vector.memset(s2[:].bitcast(I32), 0)
 
-        def load_scales(tile, row, scales):
-            rows = scales.rearrange("e s b n -> b (e s) n")
+        def load_packed(tile, scales, g):
             for q in range(4):
-                dst = tile[32 * q + row : 32 * q + row + 4, :].bitcast(I32)
                 nc.sync.dma_start(
-                    dst.rearrange("r (e n) -> r e n", e=E), rows[4 * q : 4 * q + 4].bitcast(I32)
+                    tile[32 * q : 32 * q + 4 * PLANES, g * H : (g + 1) * H].bitcast(I32),
+                    scales[PLANES * g : PLANES * (g + 1), 0, 4 * q : 4 * q + 4, :].bitcast(I32),
                 )
 
-        for q in range(4):
-            nc.sync.dma_start(
-                x_s[32 * q : 32 * q + 4, :].bitcast(I32), x_scales[0, 4 * q : 4 * q + 4, :].bitcast(I32)
-            )
+        def plane(tile, e, first, last):
+            col = e // PLANES * H
+            return tile[4 * (e % PLANES) : P, col + first : col + last]
+
+        x_rows = x_scales[0].rearrange("(q r) n -> r q n", r=4)
+        wp_rows = wp_scales.rearrange("e s (q r) n -> r q (e s) n", r=4)
         nc.sync.dma_start(tok_list[:], offs)
         nc.sync.dma_start(par_list[:], offs2)
+        for r in range(4):
+            nc.sync.dma_start(x_s[r:P:32, :].bitcast(I32), x_rows[r].bitcast(I32))
         nc.sync.dma_start(x_w[:].bitcast(I32), x_words[0].rearrange("p n d -> p (n d)").bitcast(I32))
         load_group(nc.sync, w1, w1_src, *GROUPS_1[0], "w1", U32)
-        load_scales(s1, W1_ROW, w1_scales)
-        load_scales(s1, 0, wp_scales)
+        load_packed(s1, w1_scales, 0)
+        for r in range(4):
+            nc.sync.dma_start(
+                sp[r:P:32, :].bitcast(I32).rearrange("q (e n) -> q e n", e=E), wp_rows[r].bitcast(I32)
+            )
         for g in range(1, len(GROUPS_1)):
             load_group(nc.sync, w1, w1_src, *GROUPS_1[g], "w1", U32)
             load_group(nc.sync, wp, wp_src, *GROUPS_1[g], "wp", U8)
             if g == 1:
-                load_scales(s2, W2_ROW, w2_scales)
+                load_packed(s2, w2_scales, 0)
+            if g == 2:
+                load_packed(s1, w1_scales, 1)
+                load_packed(s2, w2_scales, 1)
             load_group(nc.sync, w2, w2_src, *GROUPS_2[g - 1], "w2", U32)
 
-        work = [[psum.tile([P, H], F32, name=f"work{i}_{a}") for a in range(HALVES)] for i in range(2)]
-        res = [psum.tile([P, N], F32, name=f"res{i}") for i in range(4)]
+        words, sbytes, first, relu, turned, hidden, codes, cscales = {}, {}, {}, {}, {}, {}, {}, {}
 
-        words, sbytes, relu, hidden, codes, cscales = {}, {}, {}, {}, {}, {}
-
-        def gather_bytes(e, tag):
+        def gather_bytes(e):
             cols = slice(e * LIST_COLS, (e + 1) * LIST_COLS)
-            sbytes[e] = ring.tile([P, 2 * C], U8, name=f"bytes{e}", tag=tag, align_bytes=64)
+            sbytes[e] = ring.tile([P, 2 * C], U8, name=f"bytes{e}", tag="bytes", bufs=BYTE_RING, align_bytes=64)
             nc.vector.tensor_copy(sbytes[e][:, 0:C], x_s[:].indirect(tok_list[:, cols]))
             nc.vector.tensor_copy(sbytes[e][:, C : 2 * C], x_s[:].indirect(par_list[:, cols]))
 
         def gather_words(e):
             cols = slice(e * LIST_COLS, (e + 1) * LIST_COLS)
-            words[e] = ring.tile([P, 2 * C], U32, name=f"words{e}", tag=f"wide{e % RING}", align_bytes=64)
+            words[e] = ring.tile([P, 2 * C], U32, name=f"words{e}", tag=f"wide{e % WORD_RING}", align_bytes=64)
             nc.vector.tensor_copy(words[e][:, 0:C], x_w[:].indirect(tok_list[:, cols]))
             nc.vector.tensor_copy(words[e][:, C : 2 * C], x_w[:].indirect(par_list[:, cols]))
 
         def first_layer(e, a):
             tok = slice(a * P, (a + 1) * P)
             par = slice(C + a * P, C + (a + 1) * P)
-            cols = slice(e * H, (e + 1) * H)
+            first[e, a] = psum.tile([P, H], F32, name=f"first{e}_{a}", tag="first", bufs=FIRST_BANKS)
             nc.tensor.matmul_mx(
-                out=work[e % 2][a][:], lhsT=words[e][:, tok].bitcast(FP8X4), lhsT_scale=sbytes[e][:, tok],
-                rhs=w1[e].bitcast(FP8X4), rhs_scale=s1[W1_ROW:P, cols], start=True, stop=False,
+                out=first[e, a][:], lhsT=words[e][:, tok].bitcast(FP8X4), lhsT_scale=sbytes[e][:, tok],
+                rhs=w1[e].bitcast(FP8X4), rhs_scale=plane(s1, e, 0, H), start=True, stop=False,
             )
             nc.tensor.matmul_mx(
-                out=work[e % 2][a][:], lhsT=words[e][:, par].bitcast(FP8X4), lhsT_scale=sbytes[e][:, par],
-                rhs=wp[e].bitcast(FP4X4), rhs_scale=s1[:, cols], start=False, stop=True,
+                out=first[e, a][:], lhsT=words[e][:, par].bitcast(FP8X4), lhsT_scale=sbytes[e][:, par],
+                rhs=wp[e].bitcast(FP4X4), rhs_scale=sp[:, e * H : (e + 1) * H], start=False, stop=True,
             )
 
         def rectify(e, a):
-            tag = f"half{HALVES * e + a}"
-            relu[e, a] = ring.tile([P, PACK, P], F32, name=f"relu{e}_{a}", tag=tag, align_bytes=64)
-            src = work[e % 2][a][:].rearrange("s (g u t) -> s g t u", u=PACK, t=PACK)
-            dst = relu[e, a][:].rearrange("s t (g u) -> s g t u", u=PACK)
-            if (e, a) in VEC_RELU:
-                nc.vector.tensor_scalar_max(dst, src, 0.0)
+            relu[e, a] = ring.tile([P, PACK, P], F32, name=f"relu{e}_{a}", align_bytes=64)
+            src = first[e, a][:].rearrange("s (p t) -> s t p", t=PACK)
+            if HALVES * e + a >= VEC_RELU_FROM:
+                nc.vector.tensor_scalar_max(relu[e, a][:], src, 0.0)
             else:
-                nc.scalar.activation(dst, src, ACT.Relu)
+                nc.scalar.activation(relu[e, a][:], src, ACT.Relu)
 
         def turn(e, a):
-            bank = work[e % 2][1 - a][:].rearrange("p (t s) -> p t s", t=PACK)
+            turned[e, a] = psum.tile([P, PACK, P], F32, name=f"turned{e}_{a}", tag="turned", bufs=TURN_BANKS)
             for t in range(PACK):
-                nc.tensor.transpose(bank[:, t, :], relu[e, a][:, t, :], ident[:])
+                nc.tensor.transpose(turned[e, a][:, t, :], relu[e, a][:, t, :], ident[:])
 
         def square(e, a):
             if a == 0:
-                hidden[e] = ring.tile([P, C, PACK], BF16, name=f"hidden{e}", tag=f"wide{e % RING}", align_bytes=64)
-            bank = work[e % 2][1 - a][:].rearrange("p (t s) -> p t s", t=PACK)
+                hidden[e] = ring.tile([P, C, PACK], BF16, name=f"hidden{e}", tag=f"wide{e % WORD_RING}", align_bytes=64)
             nc.scalar.activation(
-                hidden[e][:, a * P : (a + 1) * P, :], bank.rearrange("p t s -> p s t"), ACT.Square
+                hidden[e][:, a * P : (a + 1) * P, :], turned[e, a][:].rearrange("p t s -> p s t"), ACT.Square
             )
 
-        def quantize(e, first, last):
-            if first == 0:
-                codes[e] = ring.tile([P, C], U32, name=f"codes{e}", align_bytes=64)
-                cscales[e] = ring.tile([P, C], U8, name=f"cscales{e}", align_bytes=64)
+        def quantize(e):
+            codes[e] = ring.tile([P, C], U32, name=f"codes{e}", align_bytes=64)
+            cscales[e] = ring.tile([P, C], U8, name=f"cscales{e}", align_bytes=64)
             nc.vector.quantize_mx(
-                out=codes[e][:, first:last].bitcast(FP8X4), scales=cscales[e][:, first:last],
-                in_=hidden[e][:, first:last, :].rearrange("p s t -> p (s t)"),
+                out=codes[e][:].bitcast(FP8X4), scales=cscales[e][:],
+                in_=hidden[e][:].rearrange("p s t -> p (s t)"),
             )
 
         def second_layer(e, a):
-            if e >= E - FINE:
-                blocks, slots = range(N // P), slice(a * P, (a + 1) * P)
-            else:
-                blocks, slots = range(2 * a, 2 * a + 2), slice(0, C)
-            width = slots.stop - slots.start
-            bank = res[(2 * e + a) % 4]
-            for j, block in enumerate(blocks):
-                n0 = block * P
+            bank = psum.tile([P, N], F32, name=f"result{e}_{a}", tag="result", bufs=RESULT_BANKS)
+            for j in range(2):
+                n0 = (2 * a + j) * P
                 nc.tensor.matmul_mx(
-                    out=bank[:, j * width : (j + 1) * width], lhsT=w2[e][:, n0 : n0 + P].bitcast(FP8X4),
-                    lhsT_scale=s2[W2_ROW:P, e * N + n0 : e * N + n0 + P],
-                    rhs=codes[e][:, slots].bitcast(FP8X4), rhs_scale=cscales[e][:, slots], start=True, stop=True,
+                    out=bank[:, j * C : (j + 1) * C], lhsT=w2[e][:, n0 : n0 + P].bitcast(FP8X4),
+                    lhsT_scale=plane(s2, e, n0, n0 + P),
+                    rhs=codes[e][:].bitcast(FP8X4), rhs_scale=cscales[e][:], start=True, stop=True,
                 )
             staged = ring.tile([P, N], F32, name=f"staged{e}_{a}", align_bytes=64)
-            if (e, a) in VEC_OUT:
+            if a == 0 and e >= VEC_OUT_FROM:
                 nc.vector.tensor_copy(staged[:], bank[:])
             else:
                 nc.scalar.copy(staged[:], bank[:])
-            rows = out[blocks.start * P : blocks.stop * P, e * C + slots.start : e * C + slots.stop]
+            rows = out[2 * a * P : (2 * a + 2) * P, e * C : (e + 1) * C]
             nc.sync.dma_start(
-                rows.rearrange("(j p) c -> p j c", p=P), staged[:].rearrange("p (j c) -> p j c", c=width)
+                rows.rearrange("(j p) c -> p j c", p=P), staged[:].rearrange("p (j c) -> p j c", c=C)
             )
 
-        for e in range(RING):
-            if e < EARLY:
-                gather_bytes(e, f"bytes{e % EARLY}")
+        for e in range(WORD_RING):
+            if e < BYTE_RING:
+                gather_bytes(e)
             gather_words(e)
-        for step in range(E + LAG):
-            e, late = step, step - LAG
+        for step in range(E + OUT_LAG):
+            e, mid, late = step, step - SQUARE_LAG, step - OUT_LAG
             if e < E:
                 for a in range(HALVES):
                     first_layer(e, a)
-                    if a == HALVES - 1 and e + EARLY < E:
-                        gather_bytes(e + EARLY, f"bytes{e % EARLY}")
                     rectify(e, a)
+                if e + BYTE_RING < E:
+                    gather_bytes(e + BYTE_RING)
                 for a in range(HALVES):
                     turn(e, a)
-            if late >= 0:
-                for a in range(2):
-                    second_layer(late, a)
-            if e < E:
+            if 0 <= mid < E:
                 for a in range(HALVES):
-                    square(e, a)
-                    if e >= E - FINE:
-                        quantize(e, a * P, (a + 1) * P)
-                if e < E - FINE:
-                    quantize(e, 0, C)
-                if e + RING < E:
-                    gather_words(e + RING)
+                    square(mid, a)
+                quantize(mid)
+                if mid + WORD_RING < E:
+                    gather_words(mid + WORD_RING)
+            if late >= 0:
+                for a in range(HALVES):
+                    second_layer(late, a)

@@ -22,16 +22,16 @@ PACK = 4
 HALVES = C // P
 LIST_COLS = C // 16
 PLANES = 4
-WORD_RING = 4
-BYTE_RING = 2
-FIRST_BANKS = 3
+GROUPS_1 = [(0, 2), (2, 4), (4, 6), (6, 8)]
+GROUPS_2 = [(0, 2), (2, 5), (5, 8)]
+GATHER_LEAD = 3
+FIRST_BANKS = 2
 TURN_BANKS = 2
 RESULT_BANKS = 3
-GROUPS_1 = [(0, 1), (1, 3), (3, 5), (5, 8)]
-GROUPS_2 = [(0, 2), (2, 5), (5, 8)]
-VEC_RELU_FROM = 13
-VEC_OUT_FROM = 3
-SQUARE_LAG = 1
+BYTE_SHIFT = 0
+VEC_RELU = []
+VEC_OUT = [(2, 0), (2, 1), (3, 0), (3, 1), (4, 0), (4, 1), (5, 0), (6, 0), (7, 0)]
+EARLY_RESULTS = 4
 OUT_LAG = 2
 
 
@@ -42,12 +42,14 @@ def tile_moe_duo_s_relu2_kernel(
     with ExitStack() as ctx:
         held = ctx.enter_context(tc.tile_pool(name="held", bufs=1))
         ring = ctx.enter_context(tc.tile_pool(name="ring", bufs=1))
+        work = ctx.enter_context(tc.tile_pool(name="work", bufs=1))
         psum = ctx.enter_context(tc.psum_pool(name="psum", bufs=1))
 
         tok_list = held.tile([P, E * LIST_COLS], U16, name="tok_list")
         par_list = held.tile([P, E * LIST_COLS], U16, name="par_list")
         x_w = held.tile([P, T], U32, name="x_w", align_bytes=64)
         x_s = held.tile([P, T], U8, name="x_s", align_bytes=64)
+        x_rows_in = ring.tile([P, T], U8, name="x_rows_in", tag="early", align_bytes=64)
         sp = held.tile([P, E * H], U8, name="sp", align_bytes=64)
         s1 = held.tile([P, E // PLANES * H], U8, name="s1", align_bytes=64)
         s2 = held.tile([P, E // PLANES * N], U8, name="s2", align_bytes=64)
@@ -66,16 +68,16 @@ def tile_moe_duo_s_relu2_kernel(
         wp_src = wp_words.rearrange("e s p n -> e (s p) n").bitcast(I32)
         w2_src = w2_words.rearrange("e s p n d -> e (s p) (n d)").bitcast(I32)
 
-        nc.gpsimd.memset(x_s[:].bitcast(I32), 0)
+        nc.gpsimd.memset(x_rows_in[:].bitcast(I32), 0)
+        nc.gpsimd.memset(s1[:].bitcast(I32), 0)
+        nc.gpsimd.memset(s2[:].bitcast(I32), 0)
         load_group(nc.gpsimd, wp, wp_src, *GROUPS_1[0], "wp", U8)
         make_identity(nc, ident[:])
-        nc.vector.memset(s1[:].bitcast(I32), 0)
         nc.vector.memset(sp[:].bitcast(I32), 0)
-        nc.vector.memset(s2[:].bitcast(I32), 0)
 
-        def load_packed(tile, scales, g):
+        def load_packed(queue, tile, scales, g):
             for q in range(4):
-                nc.sync.dma_start(
+                queue.dma_start(
                     tile[32 * q : 32 * q + 4 * PLANES, g * H : (g + 1) * H].bitcast(I32),
                     scales[PLANES * g : PLANES * (g + 1), 0, 4 * q : 4 * q + 4, :].bitcast(I32),
                 )
@@ -86,40 +88,45 @@ def tile_moe_duo_s_relu2_kernel(
 
         x_rows = x_scales[0].rearrange("(q r) n -> r q n", r=4)
         wp_rows = wp_scales.rearrange("e s (q r) n -> r q (e s) n", r=4)
+        nc.sync.dma_start(x_w[:].bitcast(I32), x_words[0].rearrange("p n d -> p (n d)").bitcast(I32))
         nc.sync.dma_start(tok_list[:], offs)
         nc.sync.dma_start(par_list[:], offs2)
         for r in range(4):
-            nc.sync.dma_start(x_s[r:P:32, :].bitcast(I32), x_rows[r].bitcast(I32))
-        nc.sync.dma_start(x_w[:].bitcast(I32), x_words[0].rearrange("p n d -> p (n d)").bitcast(I32))
+            nc.sync.dma_start(x_rows_in[r:P:32, :].bitcast(I32), x_rows[r].bitcast(I32))
         load_group(nc.sync, w1, w1_src, *GROUPS_1[0], "w1", U32)
-        load_packed(s1, w1_scales, 0)
+        load_packed(nc.sync, s1, w1_scales, 0)
         for r in range(4):
             nc.sync.dma_start(
                 sp[r:P:32, :].bitcast(I32).rearrange("q (e n) -> q e n", e=E), wp_rows[r].bitcast(I32)
             )
-        for g in range(1, len(GROUPS_1)):
-            load_group(nc.sync, w1, w1_src, *GROUPS_1[g], "w1", U32)
-            load_group(nc.sync, wp, wp_src, *GROUPS_1[g], "wp", U8)
-            if g == 1:
-                load_packed(s2, w2_scales, 0)
-            if g == 2:
-                load_packed(s1, w1_scales, 1)
-                load_packed(s2, w2_scales, 1)
-            load_group(nc.sync, w2, w2_src, *GROUPS_2[g - 1], "w2", U32)
+        load_group(nc.sync, w1, w1_src, *GROUPS_1[1], "w1", U32)
+        load_group(nc.sync, wp, wp_src, *GROUPS_1[1], "wp", U8)
+        load_packed(nc.sync, s2, w2_scales, 0)
+        load_group(nc.sync, w2, w2_src, *GROUPS_2[0], "w2", U32)
+        load_group(nc.sync, w1, w1_src, *GROUPS_1[2], "w1", U32)
+        load_group(nc.sync, wp, wp_src, *GROUPS_1[2], "wp", U8)
+        load_group(nc.sync, w1, w1_src, *GROUPS_1[3], "w1", U32)
+        load_group(nc.sync, wp, wp_src, *GROUPS_1[3], "wp", U8)
+        load_group(nc.sync, w2, w2_src, *GROUPS_2[1], "w2", U32)
+        load_packed(nc.sync, s2, w2_scales, 1)
+        load_group(nc.sync, w2, w2_src, *GROUPS_2[2], "w2", U32)
+        load_packed(nc.gpsimd, s1, w1_scales, 1)
 
+        held_back = {}
         words, sbytes, first, relu, turned, hidden, codes, cscales = {}, {}, {}, {}, {}, {}, {}, {}
 
-        def gather_bytes(e):
+        def gather(e):
             cols = slice(e * LIST_COLS, (e + 1) * LIST_COLS)
-            sbytes[e] = ring.tile([P, 2 * C], U8, name=f"bytes{e}", tag="bytes", bufs=BYTE_RING, align_bytes=64)
-            nc.vector.tensor_copy(sbytes[e][:, 0:C], x_s[:].indirect(tok_list[:, cols]))
-            nc.vector.tensor_copy(sbytes[e][:, C : 2 * C], x_s[:].indirect(par_list[:, cols]))
-
-        def gather_words(e):
-            cols = slice(e * LIST_COLS, (e + 1) * LIST_COLS)
-            words[e] = ring.tile([P, 2 * C], U32, name=f"words{e}", tag=f"wide{e % WORD_RING}", align_bytes=64)
+            if e in range(1, GATHER_LEAD):
+                words[e] = early_words[:, e - 1, :]
+            else:
+                tile = ring.tile([P, 2 * C], U32, name=f"words{e}", tag=f"relu{e - GATHER_LEAD}", align_bytes=64)
+                words[e] = tile[:]
+            sbytes[e] = ring.tile([P, 2 * C], U8, name=f"bytes{e}", tag=f"narrow{e - GATHER_LEAD}", align_bytes=64)
             nc.vector.tensor_copy(words[e][:, 0:C], x_w[:].indirect(tok_list[:, cols]))
+            nc.vector.tensor_copy(sbytes[e][:, 0:C], x_s[:].indirect(tok_list[:, cols]))
             nc.vector.tensor_copy(words[e][:, C : 2 * C], x_w[:].indirect(par_list[:, cols]))
+            nc.vector.tensor_copy(sbytes[e][:, C : 2 * C], x_s[:].indirect(par_list[:, cols]))
 
         def first_layer(e, a):
             tok = slice(a * P, (a + 1) * P)
@@ -135,35 +142,43 @@ def tile_moe_duo_s_relu2_kernel(
             )
 
         def rectify(e, a):
-            relu[e, a] = ring.tile([P, PACK, P], F32, name=f"relu{e}_{a}", align_bytes=64)
+            tag = f"narrow{e + BYTE_SHIFT}" if a == 1 else f"relu{e}"
+            relu[e, a] = ring.tile([P, H], F32, name=f"relu{e}_{a}", tag=tag, align_bytes=64)
+            dst = relu[e, a][:].rearrange("s (t p) -> s t p", t=PACK)
             src = first[e, a][:].rearrange("s (p t) -> s t p", t=PACK)
-            if HALVES * e + a >= VEC_RELU_FROM:
-                nc.vector.tensor_scalar_max(relu[e, a][:], src, 0.0)
+            if (e, a) in VEC_RELU:
+                nc.vector.tensor_scalar_max(dst, src, 0.0)
             else:
-                nc.scalar.activation(relu[e, a][:], src, ACT.Relu)
+                nc.scalar.activation(dst, src, ACT.Relu)
+
+        def new_hidden(e):
+            hidden[e] = ring.tile([P, C, PACK], BF16, name=f"hidden{e}", tag=f"narrow{e + 1 - GATHER_LEAD}" if e < E - 1 else "last", align_bytes=64)
 
         def turn(e, a):
             turned[e, a] = psum.tile([P, PACK, P], F32, name=f"turned{e}_{a}", tag="turned", bufs=TURN_BANKS)
             for t in range(PACK):
-                nc.tensor.transpose(turned[e, a][:, t, :], relu[e, a][:, t, :], ident[:])
+                nc.tensor.transpose(turned[e, a][:, t, :], relu[e, a][:, t * P : (t + 1) * P], ident[:])
 
         def square(e, a):
             if a == 0:
-                hidden[e] = ring.tile([P, C, PACK], BF16, name=f"hidden{e}", tag=f"wide{e % WORD_RING}", align_bytes=64)
+                new_hidden(e)
             nc.scalar.activation(
                 hidden[e][:, a * P : (a + 1) * P, :], turned[e, a][:].rearrange("p t s -> p s t"), ACT.Square
             )
 
         def quantize(e):
-            codes[e] = ring.tile([P, C], U32, name=f"codes{e}", align_bytes=64)
-            cscales[e] = ring.tile([P, C], U8, name=f"cscales{e}", align_bytes=64)
+            codes[e] = work.tile([P, C], U32, name=f"codes{e}", align_bytes=64)
+            cscales[e] = work.tile([P, C], U8, name=f"cscales{e}", align_bytes=64)
             nc.vector.quantize_mx(
                 out=codes[e][:].bitcast(FP8X4), scales=cscales[e][:],
                 in_=hidden[e][:].rearrange("p s t -> p (s t)"),
             )
 
         def second_layer(e, a):
-            bank = psum.tile([P, N], F32, name=f"result{e}_{a}", tag="result", bufs=RESULT_BANKS)
+            if HALVES * e + a < EARLY_RESULTS:
+                bank = psum.tile([P, N], F32, name=f"result{e}_{a}", tag="early_result")
+            else:
+                bank = psum.tile([P, N], F32, name=f"result{e}_{a}", tag="result", bufs=RESULT_BANKS)
             for j in range(2):
                 n0 = (2 * a + j) * P
                 nc.tensor.matmul_mx(
@@ -171,8 +186,16 @@ def tile_moe_duo_s_relu2_kernel(
                     lhsT_scale=plane(s2, e, n0, n0 + P),
                     rhs=codes[e][:].bitcast(FP8X4), rhs_scale=cscales[e][:], start=True, stop=True,
                 )
-            staged = ring.tile([P, N], F32, name=f"staged{e}_{a}", align_bytes=64)
-            if a == 0 and e >= VEC_OUT_FROM:
+            j = HALVES * e + a - EARLY_RESULTS
+            if j == 0:
+                held_back[0] = ring.tile(
+                    [P, RESULT_BANKS, N], F32, name="held_back", tag=f"relu{E - 2 - GATHER_LEAD}", align_bytes=64
+                )
+            if j in range(RESULT_BANKS):
+                staged = held_back[0][:, j, :]
+            else:
+                staged = work.tile([P, N], F32, name=f"staged{e}_{a}", align_bytes=64)
+            if (e, a) in VEC_OUT:
                 nc.vector.tensor_copy(staged[:], bank[:])
             else:
                 nc.scalar.copy(staged[:], bank[:])
@@ -181,26 +204,26 @@ def tile_moe_duo_s_relu2_kernel(
                 rows.rearrange("(j p) c -> p j c", p=P), staged[:].rearrange("p (j c) -> p j c", c=C)
             )
 
-        for e in range(WORD_RING):
-            if e < BYTE_RING:
-                gather_bytes(e)
-            gather_words(e)
-        for step in range(E + OUT_LAG):
-            e, mid, late = step, step - SQUARE_LAG, step - OUT_LAG
+        nc.vector.tensor_copy(x_s[:].bitcast(I32), x_rows_in[:].bitcast(I32))
+        early_words = ring.tile([P, GATHER_LEAD - 1, 2 * C], U32, name="early_words", tag="early", align_bytes=64)
+        for e in range(GATHER_LEAD):
+            gather(e)
+        for step in range(E + 1):
+            e, mid, late = step, step - 1, step - OUT_LAG
             if e < E:
                 for a in range(HALVES):
                     first_layer(e, a)
                     rectify(e, a)
-                if e + BYTE_RING < E:
-                    gather_bytes(e + BYTE_RING)
-                for a in range(HALVES):
-                    turn(e, a)
             if 0 <= mid < E:
+                for a in range(HALVES):
+                    turn(mid, a)
+                if mid + GATHER_LEAD < E:
+                    gather(mid + GATHER_LEAD)
                 for a in range(HALVES):
                     square(mid, a)
                 quantize(mid)
-                if mid + WORD_RING < E:
-                    gather_words(mid + WORD_RING)
-            if late >= 0:
-                for a in range(HALVES):
-                    second_layer(late, a)
+            if 0 <= late < EARLY_RESULTS:
+                second_layer(*divmod(late, HALVES))
+            if step >= E - 1:
+                for j in range(max(EARLY_RESULTS, (step - E + 1) * HALVES * mid), HALVES * step):
+                    second_layer(*divmod(j, HALVES))

@@ -32,6 +32,7 @@ BYTE_SHIFT = 0
 VEC_RELU = []
 VEC_OUT = [(2, 0), (2, 1), (3, 0), (3, 1), (4, 0), (4, 1), (5, 0), (6, 0), (7, 0)]
 EARLY_RESULTS = 4
+LATE_LAG = 3
 OUT_LAG = 2
 
 
@@ -51,7 +52,6 @@ def tile_moe_duo_s_relu2_kernel(
         x_s = held.tile([P, T], U8, name="x_s", align_bytes=64)
         x_rows_in = ring.tile([P, T], U8, name="x_rows_in", tag="early", align_bytes=64)
         sp = held.tile([P, E * H], U8, name="sp", align_bytes=64)
-        s1 = held.tile([P, E // PLANES * H], U8, name="s1", align_bytes=64)
         s2 = held.tile([P, E // PLANES * N], U8, name="s2", align_bytes=64)
         ident = held.tile([P, P], F32, name="ident", align_bytes=64)
         w1, wp, w2 = {}, {}, {}
@@ -69,11 +69,10 @@ def tile_moe_duo_s_relu2_kernel(
         w2_src = w2_words.rearrange("e s p n d -> e (s p) (n d)").bitcast(I32)
 
         nc.gpsimd.memset(x_rows_in[:].bitcast(I32), 0)
-        nc.gpsimd.memset(s1[:].bitcast(I32), 0)
-        nc.gpsimd.memset(s2[:].bitcast(I32), 0)
         load_group(nc.gpsimd, wp, wp_src, *GROUPS_1[0], "wp", U8)
         make_identity(nc, ident[:])
         nc.vector.memset(sp[:].bitcast(I32), 0)
+        nc.vector.memset(s2[:].bitcast(I32), 0)
 
         def load_packed(queue, tile, scales, g):
             for q in range(4):
@@ -87,6 +86,7 @@ def tile_moe_duo_s_relu2_kernel(
             return tile[4 * (e % PLANES) : P, col + first : col + last]
 
         x_rows = x_scales[0].rearrange("(q r) n -> r q n", r=4)
+        w1_rows = w1_scales.rearrange("e s (q r) n -> r q (e s) n", r=4)
         wp_rows = wp_scales.rearrange("e s (q r) n -> r q (e s) n", r=4)
         nc.sync.dma_start(x_w[:].bitcast(I32), x_words[0].rearrange("p n d -> p (n d)").bitcast(I32))
         nc.sync.dma_start(tok_list[:], offs)
@@ -94,25 +94,24 @@ def tile_moe_duo_s_relu2_kernel(
         for r in range(4):
             nc.sync.dma_start(x_rows_in[r:P:32, :].bitcast(I32), x_rows[r].bitcast(I32))
         load_group(nc.sync, w1, w1_src, *GROUPS_1[0], "w1", U32)
-        load_packed(nc.sync, s1, w1_scales, 0)
         for r in range(4):
-            nc.sync.dma_start(
-                sp[r:P:32, :].bitcast(I32).rearrange("q (e n) -> q e n", e=E), wp_rows[r].bitcast(I32)
-            )
+            for first_row, rows in ((4, w1_rows), (0, wp_rows)):
+                nc.sync.dma_start(
+                    sp[first_row + r : P : 32, :].bitcast(I32).rearrange("q (e n) -> q e n", e=E),
+                    rows[r].bitcast(I32),
+                )
         load_group(nc.sync, w1, w1_src, *GROUPS_1[1], "w1", U32)
         load_group(nc.sync, wp, wp_src, *GROUPS_1[1], "wp", U8)
         load_packed(nc.sync, s2, w2_scales, 0)
         load_group(nc.sync, w2, w2_src, *GROUPS_2[0], "w2", U32)
         load_group(nc.sync, w1, w1_src, *GROUPS_1[2], "w1", U32)
         load_group(nc.sync, wp, wp_src, *GROUPS_1[2], "wp", U8)
+        load_group(nc.sync, w2, w2_src, *GROUPS_2[1], "w2", U32)
         load_group(nc.sync, w1, w1_src, *GROUPS_1[3], "w1", U32)
         load_group(nc.sync, wp, wp_src, *GROUPS_1[3], "wp", U8)
-        load_group(nc.sync, w2, w2_src, *GROUPS_2[1], "w2", U32)
         load_packed(nc.sync, s2, w2_scales, 1)
         load_group(nc.sync, w2, w2_src, *GROUPS_2[2], "w2", U32)
-        load_packed(nc.gpsimd, s1, w1_scales, 1)
 
-        held_back = {}
         words, sbytes, first, relu, turned, hidden, codes, cscales = {}, {}, {}, {}, {}, {}, {}, {}
 
         def gather(e):
@@ -134,7 +133,7 @@ def tile_moe_duo_s_relu2_kernel(
             first[e, a] = psum.tile([P, H], F32, name=f"first{e}_{a}", tag="first", bufs=FIRST_BANKS)
             nc.tensor.matmul_mx(
                 out=first[e, a][:], lhsT=words[e][:, tok].bitcast(FP8X4), lhsT_scale=sbytes[e][:, tok],
-                rhs=w1[e].bitcast(FP8X4), rhs_scale=plane(s1, e, 0, H), start=True, stop=False,
+                rhs=w1[e].bitcast(FP8X4), rhs_scale=sp[4:P, e * H : (e + 1) * H], start=True, stop=False,
             )
             nc.tensor.matmul_mx(
                 out=first[e, a][:], lhsT=words[e][:, par].bitcast(FP8X4), lhsT_scale=sbytes[e][:, par],
@@ -175,10 +174,12 @@ def tile_moe_duo_s_relu2_kernel(
             )
 
         def second_layer(e, a):
-            if HALVES * e + a < EARLY_RESULTS:
-                bank = psum.tile([P, N], F32, name=f"result{e}_{a}", tag="early_result")
+            late = HALVES * e + a - EARLY_RESULTS
+            if e == E - 1:
+                bank = psum.tile([P, N], F32, name=f"result{e}_{a}", tag="first", bufs=FIRST_BANKS)
             else:
-                bank = psum.tile([P, N], F32, name=f"result{e}_{a}", tag="result", bufs=RESULT_BANKS)
+                tag = f"result{(late + 1) % (RESULT_BANKS + 1) if late >= 0 else 0}"
+                bank = psum.tile([P, N], F32, name=f"result{e}_{a}", tag=tag)
             for j in range(2):
                 n0 = (2 * a + j) * P
                 nc.tensor.matmul_mx(
@@ -186,15 +187,7 @@ def tile_moe_duo_s_relu2_kernel(
                     lhsT_scale=plane(s2, e, n0, n0 + P),
                     rhs=codes[e][:].bitcast(FP8X4), rhs_scale=cscales[e][:], start=True, stop=True,
                 )
-            j = HALVES * e + a - EARLY_RESULTS
-            if j == 0:
-                held_back[0] = ring.tile(
-                    [P, RESULT_BANKS, N], F32, name="held_back", tag=f"relu{E - 2 - GATHER_LEAD}", align_bytes=64
-                )
-            if j in range(RESULT_BANKS):
-                staged = held_back[0][:, j, :]
-            else:
-                staged = work.tile([P, N], F32, name=f"staged{e}_{a}", align_bytes=64)
+            staged = work.tile([P, N], F32, name=f"staged{e}_{a}", align_bytes=64)
             if (e, a) in VEC_OUT:
                 nc.vector.tensor_copy(staged[:], bank[:])
             else:
@@ -224,6 +217,11 @@ def tile_moe_duo_s_relu2_kernel(
                 quantize(mid)
             if 0 <= late < EARLY_RESULTS:
                 second_layer(*divmod(late, HALVES))
-            if step >= E - 1:
-                for j in range(max(EARLY_RESULTS, (step - E + 1) * HALVES * mid), HALVES * step):
-                    second_layer(*divmod(j, HALVES))
+            if step - LATE_LAG >= EARLY_RESULTS // HALVES:
+                for a in range(HALVES):
+                    second_layer(step - LATE_LAG, a)
+        for a in range(HALVES):
+            second_layer(E - 1, a)
+        for e in range(E + 1 - LATE_LAG, E - 1):
+            for a in range(HALVES):
+                second_layer(e, a)

@@ -15,25 +15,23 @@ U8 = mybir.dt.uint8
 FP8X4 = mybir.dt.float8_e4m3fn_x4
 FP4X4 = mybir.dt.float4_e2m1fn_x4
 ACT = mybir.ActivationFunctionType
-ALU = mybir.AluOpType
 
 P = 128
 PACK = 4
 HALVES = C // P
 LIST_COLS = C // 16
+QUADRANT = 32
+SCALE_ROWS = 4
 PLANES = 4
-GROUPS_1 = [(0, 2), (2, 4), (4, 6), (6, 8)]
-GROUPS_2 = [(0, 2), (2, 5), (5, 8)]
+W1_PLANE_START = 4
+PAIR = 2
+W2_LOADS = [(0, 2), (2, 5), (5, 8)]
 GATHER_LEAD = 3
-FIRST_BANKS = 2
-TURN_BANKS = 2
-RESULT_BANKS = 3
-BYTE_SHIFT = 0
-VEC_RELU = []
-VEC_OUT = [(2, 0), (2, 1), (3, 0), (3, 1), (4, 0), (4, 1), (5, 0), (6, 0), (7, 0)]
-EARLY_RESULTS = 4
-LATE_LAG = 3
-OUT_LAG = 2
+RESULT_LAG = 3
+WORK_BANKS = 2
+RESULT_BANKS = 4
+SCALAR_FIRST_RESULTS = 5
+SCALAR_AGAIN_FROM = 5
 
 
 def tile_moe_duo_s_relu2_kernel(
@@ -42,86 +40,79 @@ def tile_moe_duo_s_relu2_kernel(
     nc = tc.nc
     with ExitStack() as ctx:
         held = ctx.enter_context(tc.tile_pool(name="held", bufs=1))
-        ring = ctx.enter_context(tc.tile_pool(name="ring", bufs=1))
-        work = ctx.enter_context(tc.tile_pool(name="work", bufs=1))
+        shared = ctx.enter_context(tc.tile_pool(name="shared", bufs=1))
         psum = ctx.enter_context(tc.psum_pool(name="psum", bufs=1))
 
         tok_list = held.tile([P, E * LIST_COLS], U16, name="tok_list")
         par_list = held.tile([P, E * LIST_COLS], U16, name="par_list")
         x_w = held.tile([P, T], U32, name="x_w", align_bytes=64)
         x_s = held.tile([P, T], U8, name="x_s", align_bytes=64)
-        x_rows_in = ring.tile([P, T], U8, name="x_rows_in", tag="early", align_bytes=64)
+        x_s_landing = shared.tile([P, T], U8, name="x_s_landing", tag="start", align_bytes=64)
+        s1 = held.tile([P, E * H], U8, name="s1", align_bytes=64)
         sp = held.tile([P, E * H], U8, name="sp", align_bytes=64)
         s2 = held.tile([P, E // PLANES * N], U8, name="s2", align_bytes=64)
         ident = held.tile([P, P], F32, name="ident", align_bytes=64)
         w1, wp, w2 = {}, {}, {}
 
-        def load_group(queue, store, words, first, last, name, dtype):
-            row_words = words.shape[-1]
-            width = row_words if dtype == U32 else 4 * row_words
-            tile = held.tile([P, last - first, width], dtype, name=f"{name}_{first}", align_bytes=64)
-            queue.dma_start(tile[:].bitcast(I32), words[first:last].rearrange("e p n -> p e n"))
-            for e in range(first, last):
-                store[e] = tile[:, e - first, :]
-
         w1_src = w1_words.rearrange("e s p n d -> e (s p) (n d)").bitcast(I32)
         wp_src = wp_words.rearrange("e s p n -> e (s p) n").bitcast(I32)
         w2_src = w2_words.rearrange("e s p n d -> e (s p) (n d)").bitcast(I32)
 
-        nc.gpsimd.memset(x_rows_in[:].bitcast(I32), 0)
-        load_group(nc.gpsimd, wp, wp_src, *GROUPS_1[0], "wp", U8)
-        make_identity(nc, ident[:])
-        nc.vector.memset(sp[:].bitcast(I32), 0)
-        nc.vector.memset(s2[:].bitcast(I32), 0)
+        def load_weights(queue, store, src, first, last, name):
+            tile = held.tile([P, last - first, 4 * src.shape[-1]], U8, name=f"{name}_{first}", align_bytes=64)
+            queue.dma_start(tile[:].bitcast(I32), src[first:last].rearrange("e p n -> p e n"))
+            for e in range(first, last):
+                store[e] = tile[:, e - first, :]
 
-        def load_packed(queue, tile, scales, g):
-            for q in range(4):
-                queue.dma_start(
-                    tile[32 * q : 32 * q + 4 * PLANES, g * H : (g + 1) * H].bitcast(I32),
-                    scales[PLANES * g : PLANES * (g + 1), 0, 4 * q : 4 * q + 4, :].bitcast(I32),
+        def load_first_layer(first):
+            load_weights(nc.sync, w1, w1_src, first, first + PAIR, "w1")
+            load_weights(nc.sync, wp, wp_src, first, first + PAIR, "wp")
+
+        def load_plane_rows(tile, start, scales):
+            rows = scales.rearrange("e s (q r) n -> r q (e s) n", r=SCALE_ROWS)
+            for r in range(SCALE_ROWS):
+                dst = tile[start + r : P : QUADRANT, :].bitcast(I32).rearrange("q (e n) -> q e n", e=E)
+                nc.sync.dma_start(dst, rows[r].bitcast(I32))
+
+        def load_w2_scales(group):
+            for q in range(P // QUADRANT):
+                nc.sync.dma_start(
+                    s2[QUADRANT * q : QUADRANT * q + SCALE_ROWS * PLANES, group * N : (group + 1) * N].bitcast(I32),
+                    w2_scales[PLANES * group : PLANES * (group + 1), 0, SCALE_ROWS * q : SCALE_ROWS * (q + 1), :]
+                    .bitcast(I32),
                 )
 
-        def plane(tile, e, first, last):
-            col = e // PLANES * H
-            return tile[4 * (e % PLANES) : P, col + first : col + last]
-
-        x_rows = x_scales[0].rearrange("(q r) n -> r q n", r=4)
-        w1_rows = w1_scales.rearrange("e s (q r) n -> r q (e s) n", r=4)
-        wp_rows = wp_scales.rearrange("e s (q r) n -> r q (e s) n", r=4)
+        load_weights(nc.gpsimd, w1, w1_src, 0, PAIR, "w1")
+        make_identity(nc, ident[:])
+        for tile in (x_s_landing, s1, sp, s2):
+            nc.vector.memset(tile[:].bitcast(I32), 0)
         nc.sync.dma_start(x_w[:].bitcast(I32), x_words[0].rearrange("p n d -> p (n d)").bitcast(I32))
         nc.sync.dma_start(tok_list[:], offs)
         nc.sync.dma_start(par_list[:], offs2)
-        for r in range(4):
-            nc.sync.dma_start(x_rows_in[r:P:32, :].bitcast(I32), x_rows[r].bitcast(I32))
-        load_group(nc.sync, w1, w1_src, *GROUPS_1[0], "w1", U32)
-        for r in range(4):
-            for first_row, rows in ((4, w1_rows), (0, wp_rows)):
-                nc.sync.dma_start(
-                    sp[first_row + r : P : 32, :].bitcast(I32).rearrange("q (e n) -> q e n", e=E),
-                    rows[r].bitcast(I32),
-                )
-        load_group(nc.sync, w1, w1_src, *GROUPS_1[1], "w1", U32)
-        load_group(nc.sync, wp, wp_src, *GROUPS_1[1], "wp", U8)
-        load_packed(nc.sync, s2, w2_scales, 0)
-        load_group(nc.sync, w2, w2_src, *GROUPS_2[0], "w2", U32)
-        load_group(nc.sync, w1, w1_src, *GROUPS_1[2], "w1", U32)
-        load_group(nc.sync, wp, wp_src, *GROUPS_1[2], "wp", U8)
-        load_group(nc.sync, w2, w2_src, *GROUPS_2[1], "w2", U32)
-        load_group(nc.sync, w1, w1_src, *GROUPS_1[3], "w1", U32)
-        load_group(nc.sync, wp, wp_src, *GROUPS_1[3], "wp", U8)
-        load_packed(nc.sync, s2, w2_scales, 1)
-        load_group(nc.sync, w2, w2_src, *GROUPS_2[2], "w2", U32)
+        x_rows = x_scales[0].rearrange("(q r) n -> r q n", r=SCALE_ROWS)
+        for r in range(SCALE_ROWS):
+            nc.sync.dma_start(x_s_landing[r:P:QUADRANT, :].bitcast(I32), x_rows[r].bitcast(I32))
+        load_weights(nc.sync, wp, wp_src, 0, PAIR, "wp")
+        load_plane_rows(s1, W1_PLANE_START, w1_scales)
+        load_plane_rows(sp, 0, wp_scales)
+        load_first_layer(PAIR)
+        load_w2_scales(0)
+        load_weights(nc.sync, w2, w2_src, *W2_LOADS[0], "w2")
+        load_first_layer(2 * PAIR)
+        load_weights(nc.sync, w2, w2_src, *W2_LOADS[1], "w2")
+        load_first_layer(3 * PAIR)
+        load_w2_scales(1)
+        load_weights(nc.sync, w2, w2_src, *W2_LOADS[2], "w2")
 
         words, sbytes, first, relu, turned, hidden, codes, cscales = {}, {}, {}, {}, {}, {}, {}, {}
 
         def gather(e):
             cols = slice(e * LIST_COLS, (e + 1) * LIST_COLS)
-            if e in range(1, GATHER_LEAD):
-                words[e] = early_words[:, e - 1, :]
-            else:
-                tile = ring.tile([P, 2 * C], U32, name=f"words{e}", tag=f"relu{e - GATHER_LEAD}", align_bytes=64)
+            giver = e - GATHER_LEAD
+            if e not in words:
+                tile = shared.tile([P, 2 * C], U32, name=f"words{e}", tag=f"words{giver}", align_bytes=64)
                 words[e] = tile[:]
-            sbytes[e] = ring.tile([P, 2 * C], U8, name=f"bytes{e}", tag=f"narrow{e - GATHER_LEAD}", align_bytes=64)
+            sbytes[e] = shared.tile([P, 2 * C], U8, name=f"bytes{e}", tag=f"bytes{giver}", align_bytes=64)
             nc.vector.tensor_copy(words[e][:, 0:C], x_w[:].indirect(tok_list[:, cols]))
             nc.vector.tensor_copy(sbytes[e][:, 0:C], x_s[:].indirect(tok_list[:, cols]))
             nc.vector.tensor_copy(words[e][:, C : 2 * C], x_w[:].indirect(par_list[:, cols]))
@@ -130,98 +121,76 @@ def tile_moe_duo_s_relu2_kernel(
         def first_layer(e, a):
             tok = slice(a * P, (a + 1) * P)
             par = slice(C + a * P, C + (a + 1) * P)
-            first[e, a] = psum.tile([P, H], F32, name=f"first{e}_{a}", tag="first", bufs=FIRST_BANKS)
+            cols = slice(e * H, (e + 1) * H)
+            first[e, a] = psum.tile([P, H], F32, name=f"first{e}_{a}", tag="first", bufs=WORK_BANKS)
             nc.tensor.matmul_mx(
                 out=first[e, a][:], lhsT=words[e][:, tok].bitcast(FP8X4), lhsT_scale=sbytes[e][:, tok],
-                rhs=w1[e].bitcast(FP8X4), rhs_scale=sp[4:P, e * H : (e + 1) * H], start=True, stop=False,
+                rhs=w1[e].bitcast(FP8X4), rhs_scale=s1[W1_PLANE_START:P, cols], start=True, stop=False,
             )
             nc.tensor.matmul_mx(
                 out=first[e, a][:], lhsT=words[e][:, par].bitcast(FP8X4), lhsT_scale=sbytes[e][:, par],
-                rhs=wp[e].bitcast(FP4X4), rhs_scale=sp[:, e * H : (e + 1) * H], start=False, stop=True,
+                rhs=wp[e].bitcast(FP4X4), rhs_scale=sp[:, cols], start=False, stop=True,
             )
 
         def rectify(e, a):
-            tag = f"narrow{e + BYTE_SHIFT}" if a == 1 else f"relu{e}"
-            relu[e, a] = ring.tile([P, H], F32, name=f"relu{e}_{a}", tag=tag, align_bytes=64)
-            dst = relu[e, a][:].rearrange("s (t p) -> s t p", t=PACK)
-            src = first[e, a][:].rearrange("s (p t) -> s t p", t=PACK)
-            if (e, a) in VEC_RELU:
-                nc.vector.tensor_scalar_max(dst, src, 0.0)
-            else:
-                nc.scalar.activation(dst, src, ACT.Relu)
-
-        def new_hidden(e):
-            hidden[e] = ring.tile([P, C, PACK], BF16, name=f"hidden{e}", tag=f"narrow{e + 1 - GATHER_LEAD}" if e < E - 1 else "last", align_bytes=64)
+            tag = f"bytes{e}" if a else f"words{e}"
+            relu[e, a] = shared.tile([P, PACK, P], F32, name=f"relu{e}_{a}", tag=tag, align_bytes=64)
+            nc.scalar.activation(relu[e, a][:], first[e, a][:].rearrange("s (p t) -> s t p", t=PACK), ACT.Relu)
 
         def turn(e, a):
-            turned[e, a] = psum.tile([P, PACK, P], F32, name=f"turned{e}_{a}", tag="turned", bufs=TURN_BANKS)
+            tag = "turned" if e < E - 1 else "first"
+            turned[e, a] = psum.tile([P, PACK, P], F32, name=f"turned{e}_{a}", tag=tag, bufs=WORK_BANKS)
             for t in range(PACK):
-                nc.tensor.transpose(turned[e, a][:, t, :], relu[e, a][:, t * P : (t + 1) * P], ident[:])
+                nc.tensor.transpose(turned[e, a][:, t, :], relu[e, a][:, t, :], ident[:])
 
-        def square(e, a):
-            if a == 0:
-                new_hidden(e)
-            nc.scalar.activation(
-                hidden[e][:, a * P : (a + 1) * P, :], turned[e, a][:].rearrange("p t s -> p s t"), ACT.Square
-            )
-
-        def quantize(e):
-            codes[e] = work.tile([P, C], U32, name=f"codes{e}", align_bytes=64)
-            cscales[e] = work.tile([P, C], U8, name=f"cscales{e}", align_bytes=64)
+        def square_and_quantize(e):
+            tag = f"bytes{e + 1 - GATHER_LEAD}" if e < E - 1 else "hidden_last"
+            hidden[e] = shared.tile([P, C, PACK], BF16, name=f"hidden{e}", tag=tag, align_bytes=64)
+            for a in range(HALVES):
+                nc.scalar.activation(
+                    hidden[e][:, a * P : (a + 1) * P, :], turned[e, a][:].rearrange("p t s -> p s t"), ACT.Square
+                )
+            codes[e] = held.tile([P, C], U32, name=f"codes{e}", align_bytes=64)
+            cscales[e] = held.tile([P, C], U8, name=f"cscales{e}", align_bytes=64)
             nc.vector.quantize_mx(
-                out=codes[e][:].bitcast(FP8X4), scales=cscales[e][:],
-                in_=hidden[e][:].rearrange("p s t -> p (s t)"),
+                out=codes[e][:].bitcast(FP8X4), scales=cscales[e][:], in_=hidden[e][:].rearrange("p s t -> p (s t)")
             )
 
-        def second_layer(e, a):
-            late = HALVES * e + a - EARLY_RESULTS
-            if e == E - 1:
-                bank = psum.tile([P, N], F32, name=f"result{e}_{a}", tag="first", bufs=FIRST_BANKS)
-            else:
-                tag = f"result{(late + 1) % (RESULT_BANKS + 1) if late >= 0 else 0}"
-                bank = psum.tile([P, N], F32, name=f"result{e}_{a}", tag=tag)
+        def second_layer(e, part):
+            bank = psum.tile([P, 2, C], F32, name=f"result{e}_{part}", tag="result", bufs=RESULT_BANKS)
             for j in range(2):
-                n0 = (2 * a + j) * P
+                n0 = (2 * part + j) * P
+                col = e // PLANES * N + n0
                 nc.tensor.matmul_mx(
-                    out=bank[:, j * C : (j + 1) * C], lhsT=w2[e][:, n0 : n0 + P].bitcast(FP8X4),
-                    lhsT_scale=plane(s2, e, n0, n0 + P),
+                    out=bank[:, j, :], lhsT=w2[e][:, PACK * n0 : PACK * (n0 + P)].bitcast(FP8X4),
+                    lhsT_scale=s2[SCALE_ROWS * (e % PLANES) : P, col : col + P],
                     rhs=codes[e][:].bitcast(FP8X4), rhs_scale=cscales[e][:], start=True, stop=True,
                 )
-            staged = work.tile([P, N], F32, name=f"staged{e}_{a}", align_bytes=64)
-            if (e, a) in VEC_OUT:
-                nc.vector.tensor_copy(staged[:], bank[:])
-            else:
+            staged = held.tile([P, 2, C], F32, name=f"staged{e}_{part}", align_bytes=64)
+            if 2 * e + part < SCALAR_FIRST_RESULTS or (part == 1 and e >= SCALAR_AGAIN_FROM):
                 nc.scalar.copy(staged[:], bank[:])
-            rows = out[2 * a * P : (2 * a + 2) * P, e * C : (e + 1) * C]
-            nc.sync.dma_start(
-                rows.rearrange("(j p) c -> p j c", p=P), staged[:].rearrange("p (j c) -> p j c", c=C)
-            )
+            else:
+                nc.vector.tensor_copy(staged[:], bank[:])
+            rows = out[2 * part * P : (2 * part + 2) * P, e * C : (e + 1) * C]
+            nc.sync.dma_start(rows.rearrange("(j p) c -> p j c", p=P), staged[:])
 
-        nc.vector.tensor_copy(x_s[:].bitcast(I32), x_rows_in[:].bitcast(I32))
-        early_words = ring.tile([P, GATHER_LEAD - 1, 2 * C], U32, name="early_words", tag="early", align_bytes=64)
+        nc.vector.tensor_copy(x_s[:].bitcast(I32), x_s_landing[:].bitcast(I32))
+        early_words = shared.tile([P, GATHER_LEAD - 1, 2 * C], U32, name="early_words", tag="start", align_bytes=64)
+        for e in range(1, GATHER_LEAD):
+            words[e] = early_words[:, e - 1, :]
         for e in range(GATHER_LEAD):
             gather(e)
-        for step in range(E + 1):
-            e, mid, late = step, step - 1, step - OUT_LAG
-            if e < E:
+        for step in range(E + RESULT_LAG):
+            if step < E:
                 for a in range(HALVES):
-                    first_layer(e, a)
-                    rectify(e, a)
-            if 0 <= mid < E:
+                    first_layer(step, a)
+                    rectify(step, a)
+            if 1 <= step <= E:
                 for a in range(HALVES):
-                    turn(mid, a)
-                if mid + GATHER_LEAD < E:
-                    gather(mid + GATHER_LEAD)
-                for a in range(HALVES):
-                    square(mid, a)
-                quantize(mid)
-            if 0 <= late < EARLY_RESULTS:
-                second_layer(*divmod(late, HALVES))
-            if step - LATE_LAG >= EARLY_RESULTS // HALVES:
-                for a in range(HALVES):
-                    second_layer(step - LATE_LAG, a)
-        for a in range(HALVES):
-            second_layer(E - 1, a)
-        for e in range(E + 1 - LATE_LAG, E - 1):
-            for a in range(HALVES):
-                second_layer(e, a)
+                    turn(step - 1, a)
+                if step - 1 + GATHER_LEAD < E:
+                    gather(step - 1 + GATHER_LEAD)
+                square_and_quantize(step - 1)
+            if step >= RESULT_LAG:
+                for part in range(2):
+                    second_layer(step - RESULT_LAG, part)

@@ -82,9 +82,10 @@ def tile_moe_duo_s_relu2_kernel(
                     .bitcast(I32),
                 )
 
-        load_weights(nc.gpsimd, w1, w1_src, 0, PAIR, "w1")
+        nc.gpsimd.memset(x_s_landing[:].bitcast(I32), 0)
+        load_weights(nc.gpsimd, w1, w1_src, 0, 1, "w1")
         make_identity(nc, ident[:])
-        for tile in (x_s_landing, s1, sp, s2):
+        for tile in (s1, sp, s2):
             nc.vector.memset(tile[:].bitcast(I32), 0)
         nc.sync.dma_start(x_w[:].bitcast(I32), x_words[0].rearrange("p n d -> p (n d)").bitcast(I32))
         nc.sync.dma_start(tok_list[:], offs)
@@ -95,6 +96,7 @@ def tile_moe_duo_s_relu2_kernel(
         load_weights(nc.sync, wp, wp_src, 0, PAIR, "wp")
         load_plane_rows(s1, W1_PLANE_START, w1_scales)
         load_plane_rows(sp, 0, wp_scales)
+        load_weights(nc.sync, w1, w1_src, 1, PAIR, "w1")
         load_first_layer(PAIR)
         load_w2_scales(0)
         load_weights(nc.sync, w2, w2_src, *W2_LOADS[0], "w2")

@@ -26,12 +26,11 @@ PLANES = 4
 W1_PLANE_START = 4
 PAIR = 2
 W2_LOADS = [(0, 2), (2, 5), (5, 8)]
-GATHER_LEAD = 3
-RESULT_LAG = 3
-WORK_BANKS = 2
-RESULT_BANKS = 4
-SCALAR_FIRST_RESULTS = 5
-SCALAR_AGAIN_FROM = 5
+MULT = mybir.AluOpType.mult
+MAX = mybir.AluOpType.max
+PAIRED_EXPERTS = E - 2
+FREE_GATHERS = 14
+GROUP = 5
 
 
 def tile_moe_duo_s_relu2_kernel(
@@ -97,102 +96,174 @@ def tile_moe_duo_s_relu2_kernel(
         load_plane_rows(s1, W1_PLANE_START, w1_scales)
         load_plane_rows(sp, 0, wp_scales)
         load_weights(nc.sync, w1, w1_src, 1, PAIR, "w1")
-        load_first_layer(PAIR)
+        load_weights(nc.sync, w1, w1_src, 2, 3, "w1")
+        load_weights(nc.sync, wp, wp_src, 2, 4, "wp")
         load_w2_scales(0)
         load_weights(nc.sync, w2, w2_src, *W2_LOADS[0], "w2")
+        load_weights(nc.sync, w1, w1_src, 3, 4, "w1")
         load_first_layer(2 * PAIR)
         load_weights(nc.sync, w2, w2_src, *W2_LOADS[1], "w2")
         load_first_layer(3 * PAIR)
         load_w2_scales(1)
         load_weights(nc.sync, w2, w2_src, *W2_LOADS[2], "w2")
 
-        words, sbytes, first, relu, turned, hidden, codes, cscales = {}, {}, {}, {}, {}, {}, {}, {}
+        gathered, first, relu, squared, turned, hidden, codes, cscales = ({} for i in range(8))
 
-        def gather(e):
-            cols = slice(e * LIST_COLS, (e + 1) * LIST_COLS)
-            giver = e - GATHER_LEAD
-            if e not in words:
-                tile = shared.tile([P, 2 * C], U32, name=f"words{e}", tag=f"words{giver}", align_bytes=64)
-                words[e] = tile[:]
-            sbytes[e] = shared.tile([P, 2 * C], U8, name=f"bytes{e}", tag=f"bytes{giver}", align_bytes=64)
-            nc.vector.tensor_copy(words[e][:, 0:C], x_w[:].indirect(tok_list[:, cols]))
-            nc.vector.tensor_copy(sbytes[e][:, 0:C], x_s[:].indirect(tok_list[:, cols]))
-            nc.vector.tensor_copy(words[e][:, C : 2 * C], x_w[:].indirect(par_list[:, cols]))
-            nc.vector.tensor_copy(sbytes[e][:, C : 2 * C], x_s[:].indirect(par_list[:, cols]))
+        def sbuf(shape, dtype, name, tag):
+            return shared.tile(shape, dtype, name=name, tag=tag, align_bytes=64)
 
-        def first_layer(e, a):
-            tok = slice(a * P, (a + 1) * P)
-            par = slice(C + a * P, C + (a + 1) * P)
+        def gather(n, tag):
+            if n >= PACK * E:
+                return
+            e, part = divmod(n, 4)
+            window, dtype = (x_w, U32) if part < 2 else (x_s, U8)
+            offsets = (tok_list, par_list)[part % 2][:, e * LIST_COLS : (e + 1) * LIST_COLS]
+            if n not in gathered:
+                gathered[n] = sbuf([P, C], dtype, f"gathered{n}", tag)[:]
+            nc.vector.tensor_copy(gathered[n], window[:].indirect(offsets))
+
+        def held_gather(k, j):
+            gather(FREE_GATHERS + GROUP * k + j, f"after{k - 1}" if j == 2 else f"hand{k}_{j}")
+
+        def bank(shape, name, tag):
+            return psum.tile(shape, F32, name=name, tag=tag)
+
+        def first_layer(e, a, tag):
             cols = slice(e * H, (e + 1) * H)
-            first[e, a] = psum.tile([P, H], F32, name=f"first{e}_{a}", tag="first", bufs=WORK_BANKS)
+            slots = slice(a * P, (a + 1) * P)
+            tok, par, tok_s, par_s = (gathered[4 * e + part][:, slots] for part in range(4))
+            first[e, a] = bank([P, H], f"first{e}_{a}", tag)
             nc.tensor.matmul_mx(
-                out=first[e, a][:], lhsT=words[e][:, tok].bitcast(FP8X4), lhsT_scale=sbytes[e][:, tok],
+                out=first[e, a][:], lhsT=tok.bitcast(FP8X4), lhsT_scale=tok_s,
                 rhs=w1[e].bitcast(FP8X4), rhs_scale=s1[W1_PLANE_START:P, cols], start=True, stop=False,
             )
             nc.tensor.matmul_mx(
-                out=first[e, a][:], lhsT=words[e][:, par].bitcast(FP8X4), lhsT_scale=sbytes[e][:, par],
+                out=first[e, a][:], lhsT=par.bitcast(FP8X4), lhsT_scale=par_s,
                 rhs=wp[e].bitcast(FP4X4), rhs_scale=sp[:, cols], start=False, stop=True,
             )
 
+        def paired(e, a):
+            return a == 0 and e < PAIRED_EXPERTS
+
         def rectify(e, a):
-            tag = f"bytes{e}" if a else f"words{e}"
-            relu[e, a] = shared.tile([P, PACK, P], F32, name=f"relu{e}_{a}", tag=tag, align_bytes=64)
-            nc.scalar.activation(relu[e, a][:], first[e, a][:].rearrange("s (p t) -> s t p", t=PACK), ACT.Relu)
+            relu[e, a] = sbuf([P, H], F32, f"relu{e}_{a}", f"hand{e - 1}_0" if a else f"hand{e - 2}_4")
+            if paired(e, a):
+                dst = relu[e, a][:].rearrange("s (u p d) -> s u p d", u=2, d=2)
+                src = first[e, a][:].rearrange("s (p u d) -> s u p d", u=2, d=2)
+            else:
+                dst = relu[e, a][:].rearrange("s (t p) -> s t p", t=PACK)
+                src = first[e, a][:].rearrange("s (p t) -> s t p", t=PACK)
+            if e >= E - 2:
+                nc.vector.tensor_scalar(dst, src, 0.0, None, MAX)
+            else:
+                nc.scalar.activation(dst, src, ACT.Relu)
 
-        def turn(e, a):
-            tag = "turned" if e < E - 1 else "first"
-            turned[e, a] = psum.tile([P, PACK, P], F32, name=f"turned{e}_{a}", tag=tag, bufs=WORK_BANKS)
+        def square_pairs(e):
+            squared[e] = sbuf([P, H], BF16, f"squared{e}", f"after{e - 2}")
+            nc.gpsimd.tensor_tensor(squared[e][:], relu[e, 0][:], relu[e, 0][:], MULT)
+
+        def hidden_tile(e, a):
+            hidden[e, a] = sbuf([P, P * PACK], BF16, f"hidden{e}_{a}", f"hand{e}_1" if a else f"after{e}")
+            return hidden[e, a]
+
+        def turn_pairs(e):
+            turned[e, 0] = bank([P, 2, P], f"turned{e}_0", "turned0")
+            pairs = squared[e][:].bitcast(F32)
+            for u in range(2):
+                nc.tensor.transpose(turned[e, 0][:, u, :], pairs[:, u * P : (u + 1) * P], ident[:])
+
+        def copy_pairs(e):
+            dst = hidden_tile(e, 0)[:].bitcast(F32).rearrange("p (s u) -> p s u", u=2)
+            nc.scalar.copy(dst, turned[e, 0][:].rearrange("p u s -> p s u"))
+
+        def turn_values(e, a, tag):
+            turned[e, a] = bank([P, PACK, P], f"turned{e}_{a}", tag)
             for t in range(PACK):
-                nc.tensor.transpose(turned[e, a][:, t, :], relu[e, a][:, t, :], ident[:])
+                nc.tensor.transpose(turned[e, a][:, t, :], relu[e, a][:, t * P : (t + 1) * P], ident[:])
 
-        def square_and_quantize(e):
-            tag = f"bytes{e + 1 - GATHER_LEAD}" if e < E - 1 else "hidden_last"
-            hidden[e] = shared.tile([P, C, PACK], BF16, name=f"hidden{e}", tag=tag, align_bytes=64)
-            for a in range(HALVES):
-                nc.scalar.activation(
-                    hidden[e][:, a * P : (a + 1) * P, :], turned[e, a][:].rearrange("p t s -> p s t"), ACT.Square
-                )
-            codes[e] = held.tile([P, C], U32, name=f"codes{e}", align_bytes=64)
+        def square_values(e, a):
+            dst = hidden_tile(e, a)[:].rearrange("p (s t) -> p s t", t=PACK)
+            nc.scalar.activation(dst, turned[e, a][:].rearrange("p t s -> p s t"), ACT.Square)
+
+        def quantize(e):
+            codes[e] = sbuf([P, C], U32, f"codes{e}", f"hand{e}_3")
             cscales[e] = held.tile([P, C], U8, name=f"cscales{e}", align_bytes=64)
-            nc.vector.quantize_mx(
-                out=codes[e][:].bitcast(FP8X4), scales=cscales[e][:], in_=hidden[e][:].rearrange("p s t -> p (s t)")
-            )
+            for a in range(HALVES):
+                cols = slice(a * P, (a + 1) * P)
+                nc.vector.quantize_mx(out=codes[e][:, cols].bitcast(FP8X4), scales=cscales[e][:, cols], in_=hidden[e, a][:])
 
-        def second_layer(e, part):
-            bank = psum.tile([P, 2, C], F32, name=f"result{e}_{part}", tag="result", bufs=RESULT_BANKS)
+        def second_layer(e, part, tag, copy):
+            result = bank([P, 2, C], f"result{e}_{part}", tag)
             for j in range(2):
                 n0 = (2 * part + j) * P
                 col = e // PLANES * N + n0
                 nc.tensor.matmul_mx(
-                    out=bank[:, j, :], lhsT=w2[e][:, PACK * n0 : PACK * (n0 + P)].bitcast(FP8X4),
+                    out=result[:, j, :], lhsT=w2[e][:, PACK * n0 : PACK * (n0 + P)].bitcast(FP8X4),
                     lhsT_scale=s2[SCALE_ROWS * (e % PLANES) : P, col : col + P],
                     rhs=codes[e][:].bitcast(FP8X4), rhs_scale=cscales[e][:], start=True, stop=True,
                 )
             staged = held.tile([P, 2, C], F32, name=f"staged{e}_{part}", align_bytes=64)
-            if 2 * e + part < SCALAR_FIRST_RESULTS or (part == 1 and e >= SCALAR_AGAIN_FROM):
-                nc.scalar.copy(staged[:], bank[:])
-            else:
-                nc.vector.tensor_copy(staged[:], bank[:])
+            copy(staged[:], result[:])
             rows = out[2 * part * P : (2 * part + 2) * P, e * C : (e + 1) * C]
             nc.sync.dma_start(rows.rearrange("(j p) c -> p j c", p=P), staged[:])
 
         nc.vector.tensor_copy(x_s[:].bitcast(I32), x_s_landing[:].bitcast(I32))
-        early_words = shared.tile([P, GATHER_LEAD - 1, 2 * C], U32, name="early_words", tag="start", align_bytes=64)
-        for e in range(1, GATHER_LEAD):
-            words[e] = early_words[:, e - 1, :]
-        for e in range(GATHER_LEAD):
-            gather(e)
-        for step in range(E + RESULT_LAG):
-            if step < E:
-                for a in range(HALVES):
-                    first_layer(step, a)
-                    rectify(step, a)
-            if 1 <= step <= E:
-                for a in range(HALVES):
-                    turn(step - 1, a)
-                if step - 1 + GATHER_LEAD < E:
-                    gather(step - 1 + GATHER_LEAD)
-                square_and_quantize(step - 1)
-            if step >= RESULT_LAG:
+        early = [n for n in range(4, FREE_GATHERS) if n % 4 < 2]
+        early_words = sbuf([P, len(early), C], U32, "early_words", "start")
+        for j, n in enumerate(early):
+            gathered[n] = early_words[:, j, :]
+        for n in range(FREE_GATHERS):
+            gather(n, f"free{n}")
+        for e in range(PAIRED_EXPERTS):
+            k = e - 2
+            for a in range(HALVES):
+                first_layer(e, a, f"first{a}")
+                rectify(e, a)
+            if k >= 0:
+                quantize(k)
+            square_pairs(e)
+            if e >= 1:
+                turn_values(e - 1, 1, "turned1")
+                turn_pairs(e - 1)
+            if k >= 0:
+                for j in range(3):
+                    held_gather(k, j)
+            if e >= 1:
+                square_values(e - 1, 1)
+                copy_pairs(e - 1)
+            if k >= 0:
                 for part in range(2):
-                    second_layer(step - RESULT_LAG, part)
+                    second_layer(k, part, f"result{k % 2}_{part}", nc.scalar.copy)
+                held_gather(k, 3)
+                held_gather(k, 4)
+        last = E - 1
+        quantize(last - 3)
+        for a in range(HALVES):
+            first_layer(last - 1, a, f"first{a}")
+        turn_values(last - 2, 1, "turned1")
+        turn_pairs(last - 2)
+        for a in range(HALVES):
+            first_layer(last, a, f"result1_{a}")
+        square_values(last - 2, 1)
+        copy_pairs(last - 2)
+        for a in range(HALVES):
+            rectify(last - 1, a)
+        for part in range(2):
+            second_layer(last - 3, part, f"result0_{part}", nc.scalar.copy)
+        quantize(last - 2)
+        for a in range(HALVES):
+            turn_values(last - 1, a, f"turned{a}")
+            square_values(last - 1, a)
+        for a in range(HALVES):
+            rectify(last, a)
+        second_layer(last - 2, 0, "result1_0", nc.vector.tensor_copy)
+        quantize(last - 1)
+        second_layer(last - 2, 1, "result1_1", nc.vector.tensor_copy)
+        for a in range(HALVES):
+            turn_values(last, a, f"first{a}")
+            square_values(last, a)
+        second_layer(last - 1, 1, "result0_1", nc.scalar.copy)
+        quantize(last)
+        second_layer(last - 1, 0, "result0_0", nc.vector.tensor_copy)
+        second_layer(last, 0, "turned0", nc.vector.tensor_copy)
+        second_layer(last, 1, "turned1", nc.scalar.copy)

@@ -28,9 +28,8 @@ PAIR = 2
 W2_LOADS = [(0, 2), (2, 5), (5, 8)]
 MULT = mybir.AluOpType.mult
 MAX = mybir.AluOpType.max
-PAIRED_EXPERTS = E - 2
-FREE_GATHERS = 14
-GROUP = 5
+PAIRED_EXPERTS = E - 1
+GROUPS = (4, 4, 5, 1)
 
 
 def tile_moe_duo_s_relu2_kernel(
@@ -46,7 +45,6 @@ def tile_moe_duo_s_relu2_kernel(
         par_list = held.tile([P, E * LIST_COLS], U16, name="par_list")
         x_w = held.tile([P, T], U32, name="x_w", align_bytes=64)
         x_s = held.tile([P, T], U8, name="x_s", align_bytes=64)
-        x_s_landing = shared.tile([P, T], U8, name="x_s_landing", tag="start", align_bytes=64)
         s1 = held.tile([P, E * H], U8, name="s1", align_bytes=64)
         sp = held.tile([P, E * H], U8, name="sp", align_bytes=64)
         s2 = held.tile([P, E // PLANES * N], U8, name="s2", align_bytes=64)
@@ -81,20 +79,20 @@ def tile_moe_duo_s_relu2_kernel(
                     .bitcast(I32),
                 )
 
-        nc.gpsimd.memset(x_s_landing[:].bitcast(I32), 0)
+        nc.gpsimd.memset(x_s[:].bitcast(I32), 0)
         load_weights(nc.gpsimd, w1, w1_src, 0, 1, "w1")
         make_identity(nc, ident[:])
-        for tile in (s1, sp, s2):
+        for tile in (sp, s1, s2):
             nc.vector.memset(tile[:].bitcast(I32), 0)
-        nc.sync.dma_start(x_w[:].bitcast(I32), x_words[0].rearrange("p n d -> p (n d)").bitcast(I32))
         nc.sync.dma_start(tok_list[:], offs)
         nc.sync.dma_start(par_list[:], offs2)
         x_rows = x_scales[0].rearrange("(q r) n -> r q n", r=SCALE_ROWS)
         for r in range(SCALE_ROWS):
-            nc.sync.dma_start(x_s_landing[r:P:QUADRANT, :].bitcast(I32), x_rows[r].bitcast(I32))
+            nc.sync.dma_start(x_s[r:P:QUADRANT, :].bitcast(I32), x_rows[r].bitcast(I32))
+        nc.sync.dma_start(x_w[:].bitcast(I32), x_words[0].rearrange("p n d -> p (n d)").bitcast(I32))
         load_weights(nc.sync, wp, wp_src, 0, PAIR, "wp")
-        load_plane_rows(s1, W1_PLANE_START, w1_scales)
         load_plane_rows(sp, 0, wp_scales)
+        load_plane_rows(s1, W1_PLANE_START, w1_scales)
         load_weights(nc.sync, w1, w1_src, 1, PAIR, "w1")
         load_weights(nc.sync, w1, w1_src, 2, 3, "w1")
         load_weights(nc.sync, wp, wp_src, 2, 4, "wp")
@@ -112,26 +110,41 @@ def tile_moe_duo_s_relu2_kernel(
         def sbuf(shape, dtype, name, tag):
             return shared.tile(shape, dtype, name=name, tag=tag, align_bytes=64)
 
+        def gather_into(dst, part, first_col, cols):
+            window = x_s if part < 2 else x_w
+            offsets = (tok_list, par_list)[part % 2][:, first_col : first_col + cols]
+            nc.vector.tensor_copy(dst, window[:].indirect(offsets))
+
         def gather(n, tag):
-            if n >= PACK * E:
-                return
             e, part = divmod(n, 4)
-            window, dtype = (x_w, U32) if part < 2 else (x_s, U8)
-            offsets = (tok_list, par_list)[part % 2][:, e * LIST_COLS : (e + 1) * LIST_COLS]
-            if n not in gathered:
-                gathered[n] = sbuf([P, C], dtype, f"gathered{n}", tag)[:]
-            nc.vector.tensor_copy(gathered[n], window[:].indirect(offsets))
+            tile = sbuf([P, C], U8 if part < 2 else U32, f"gathered{n}", tag)
+            gather_into(tile[:], part, e * LIST_COLS, LIST_COLS)
+            for a in range(HALVES):
+                gathered[e, a, part] = tile[:, a * P : (a + 1) * P]
+
+        def gather_half(a, sort, tag):
+            tile = sbuf([P, 2, P], U32 if sort else U8, f"gathered_half{a}_{sort}", tag)
+            for j in range(2):
+                gathered[E - 1, a, 2 * sort + j] = tile[:, j, :]
+                gather_into(tile[:, j, :], 2 * sort + j, (E - 1) * LIST_COLS + a * P // 16, P // 16)
+
+        def hand(k, j):
+            return f"after{k - 1}" if j == 2 else f"hand{k}_{j}"
+
+        held_order = [12, 13] + list(range(16, 4 * E))
 
         def held_gather(k, j):
-            gather(FREE_GATHERS + GROUP * k + j, f"after{k - 1}" if j == 2 else f"hand{k}_{j}")
+            if j < GROUPS[k]:
+                gather(held_order[sum(GROUPS[:k]) + j], hand(k, j))
+            elif k == len(GROUPS) - 1 and j < 3:
+                gather_half(0, j - 1, hand(k, j))
 
         def bank(shape, name, tag):
             return psum.tile(shape, F32, name=name, tag=tag)
 
         def first_layer(e, a, tag):
             cols = slice(e * H, (e + 1) * H)
-            slots = slice(a * P, (a + 1) * P)
-            tok, par, tok_s, par_s = (gathered[4 * e + part][:, slots] for part in range(4))
+            tok_s, par_s, tok, par = (gathered[e, a, part] for part in range(4))
             first[e, a] = bank([P, H], f"first{e}_{a}", tag)
             nc.tensor.matmul_mx(
                 out=first[e, a][:], lhsT=tok.bitcast(FP8X4), lhsT_scale=tok_s,
@@ -145,15 +158,20 @@ def tile_moe_duo_s_relu2_kernel(
         def paired(e, a):
             return a == 0 and e < PAIRED_EXPERTS
 
+        def relu_tag(e, a):
+            if e == E - 2:
+                return f"hand{e - 2}_4" if a == 0 else f"hand{e - 1}_1"
+            return f"hand{e - 1}_1" if a else f"hand{e - 2}_4"
+
         def rectify(e, a):
-            relu[e, a] = sbuf([P, H], F32, f"relu{e}_{a}", f"hand{e - 1}_0" if a else f"hand{e - 2}_4")
+            relu[e, a] = sbuf([P, H], F32, f"relu{e}_{a}", relu_tag(e, a))
             if paired(e, a):
                 dst = relu[e, a][:].rearrange("s (u p d) -> s u p d", u=2, d=2)
                 src = first[e, a][:].rearrange("s (p u d) -> s u p d", u=2, d=2)
             else:
                 dst = relu[e, a][:].rearrange("s (t p) -> s t p", t=PACK)
                 src = first[e, a][:].rearrange("s (p t) -> s t p", t=PACK)
-            if e >= E - 2:
+            if e == E - 1 or (e, a) == (E - 2, 0):
                 nc.vector.tensor_scalar(dst, src, 0.0, None, MAX)
             else:
                 nc.scalar.activation(dst, src, ACT.Relu)
@@ -163,18 +181,18 @@ def tile_moe_duo_s_relu2_kernel(
             nc.gpsimd.tensor_tensor(squared[e][:], relu[e, 0][:], relu[e, 0][:], MULT)
 
         def hidden_tile(e, a):
-            hidden[e, a] = sbuf([P, P * PACK], BF16, f"hidden{e}_{a}", f"hand{e}_1" if a else f"after{e}")
+            hidden[e, a] = sbuf([P, P * PACK], BF16, f"hidden{e}_{a}", f"hand{e}_0" if a else f"after{e}")
             return hidden[e, a]
 
-        def turn_pairs(e):
-            turned[e, 0] = bank([P, 2, P], f"turned{e}_0", "turned0")
+        def turn_pairs(e, tag):
+            turned[e, 0] = bank([P, 2, P], f"turned{e}_0", tag)
             pairs = squared[e][:].bitcast(F32)
             for u in range(2):
                 nc.tensor.transpose(turned[e, 0][:, u, :], pairs[:, u * P : (u + 1) * P], ident[:])
 
-        def copy_pairs(e):
+        def copy_pairs(e, copy):
             dst = hidden_tile(e, 0)[:].bitcast(F32).rearrange("p (s u) -> p s u", u=2)
-            nc.scalar.copy(dst, turned[e, 0][:].rearrange("p u s -> p s u"))
+            copy(dst, turned[e, 0][:].rearrange("p u s -> p s u"))
 
         def turn_values(e, a, tag):
             turned[e, a] = bank([P, PACK, P], f"turned{e}_{a}", tag)
@@ -192,7 +210,7 @@ def tile_moe_duo_s_relu2_kernel(
                 cols = slice(a * P, (a + 1) * P)
                 nc.vector.quantize_mx(out=codes[e][:, cols].bitcast(FP8X4), scales=cscales[e][:, cols], in_=hidden[e, a][:])
 
-        def second_layer(e, part, tag, copy):
+        def second_layer(e, part, tag):
             result = bank([P, 2, C], f"result{e}_{part}", tag)
             for j in range(2):
                 n0 = (2 * part + j) * P
@@ -202,68 +220,82 @@ def tile_moe_duo_s_relu2_kernel(
                     lhsT_scale=s2[SCALE_ROWS * (e % PLANES) : P, col : col + P],
                     rhs=codes[e][:].bitcast(FP8X4), rhs_scale=cscales[e][:], start=True, stop=True,
                 )
+            return result
+
+        def store(e, part, result, copy):
             staged = held.tile([P, 2, C], F32, name=f"staged{e}_{part}", align_bytes=64)
             copy(staged[:], result[:])
             rows = out[2 * part * P : (2 * part + 2) * P, e * C : (e + 1) * C]
             nc.sync.dma_start(rows.rearrange("(j p) c -> p j c", p=P), staged[:])
 
-        nc.vector.tensor_copy(x_s[:].bitcast(I32), x_s_landing[:].bitcast(I32))
-        early = [n for n in range(4, FREE_GATHERS) if n % 4 < 2]
-        early_words = sbuf([P, len(early), C], U32, "early_words", "start")
-        for j, n in enumerate(early):
-            gathered[n] = early_words[:, j, :]
-        for n in range(FREE_GATHERS):
+        for n in range(8):
             gather(n, f"free{n}")
-        for e in range(PAIRED_EXPERTS):
+        for n in (10, 11):
+            gather(n, f"free{n}")
+        for e in range(E - 2):
             k = e - 2
             for a in range(HALVES):
-                first_layer(e, a, f"first{a}")
+                first_layer(e, a, f"result1_{a}" if e == 0 else f"first{a}")
                 rectify(e, a)
+            if e == 0:
+                for n, giver in ((8, 0), (9, 2), (14, 1), (15, 3)):
+                    gather(n, f"free{giver}")
             if k >= 0:
                 quantize(k)
             square_pairs(e)
             if e >= 1:
                 turn_values(e - 1, 1, "turned1")
-                turn_pairs(e - 1)
+                turn_pairs(e - 1, "turned0")
             if k >= 0:
                 for j in range(3):
                     held_gather(k, j)
             if e >= 1:
                 square_values(e - 1, 1)
-                copy_pairs(e - 1)
+                copy_pairs(e - 1, nc.scalar.copy)
             if k >= 0:
-                for part in range(2):
-                    second_layer(k, part, f"result{k % 2}_{part}", nc.scalar.copy)
+                banks = [second_layer(k, part, f"result{k % 2}_{part}") for part in range(2)]
                 held_gather(k, 3)
                 held_gather(k, 4)
+                store(k, 0, banks[0], nc.scalar.copy)
+                store(k, 1, banks[1], nc.scalar.copy)
+
+        def finish(e, part, tag, copy):
+            store(e, part, second_layer(e, part, tag), copy)
+
+        on_scalar, on_vector = nc.scalar.copy, nc.vector.tensor_copy
         last = E - 1
-        quantize(last - 3)
         for a in range(HALVES):
             first_layer(last - 1, a, f"first{a}")
+        rectify(last - 1, 0)
+        quantize(last - 3)
         turn_values(last - 2, 1, "turned1")
-        turn_pairs(last - 2)
-        for a in range(HALVES):
-            first_layer(last, a, f"result1_{a}")
+        turn_pairs(last - 2, "turned0")
+        for sort in range(2):
+            gather_half(1, sort, hand(last - 3, sort))
+        square_pairs(last - 1)
+        first_layer(last, 0, "result1_0")
         square_values(last - 2, 1)
-        copy_pairs(last - 2)
-        for a in range(HALVES):
-            rectify(last - 1, a)
+        copy_pairs(last - 2, on_scalar)
+        rectify(last - 1, 1)
         for part in range(2):
-            second_layer(last - 3, part, f"result0_{part}", nc.scalar.copy)
+            finish(last - 3, part, f"result0_{part}", on_scalar)
+        first_layer(last, 1, "result1_1")
+        rectify(last, 0)
         quantize(last - 2)
-        for a in range(HALVES):
-            turn_values(last - 1, a, f"turned{a}")
-            square_values(last - 1, a)
-        for a in range(HALVES):
-            rectify(last, a)
-        second_layer(last - 2, 0, "result1_0", nc.vector.tensor_copy)
+        rectify(last, 1)
+        turn_values(last - 1, 1, "turned1")
+        turn_values(last, 0, "first0")
+        turn_pairs(last - 1, "turned0")
+        turn_values(last, 1, "first1")
+        square_values(last - 1, 1)
+        copy_pairs(last - 1, on_vector)
+        finish(last - 2, 0, "result0_0", on_vector)
         quantize(last - 1)
-        second_layer(last - 2, 1, "result1_1", nc.vector.tensor_copy)
+        finish(last - 2, 1, "result0_1", on_vector)
         for a in range(HALVES):
-            turn_values(last, a, f"first{a}")
             square_values(last, a)
-        second_layer(last - 1, 1, "result0_1", nc.scalar.copy)
         quantize(last)
-        second_layer(last - 1, 0, "result0_0", nc.vector.tensor_copy)
-        second_layer(last, 0, "turned0", nc.vector.tensor_copy)
-        second_layer(last, 1, "turned1", nc.scalar.copy)
+        finish(last - 1, 0, "result1_0", on_vector)
+        finish(last - 1, 1, "result1_1", on_scalar)
+        finish(last, 0, "turned0", on_vector)
+        finish(last, 1, "turned1", on_scalar)

@@ -29,7 +29,6 @@ W2_LOADS = [(0, 2), (2, 5), (5, 8)]
 MULT = mybir.AluOpType.mult
 MAX = mybir.AluOpType.max
 PAIRED_EXPERTS = E - 1
-GROUPS = (4, 4, 5, 1)
 
 
 def tile_moe_duo_s_relu2_kernel(
@@ -45,7 +44,8 @@ def tile_moe_duo_s_relu2_kernel(
         par_list = held.tile([P, E * LIST_COLS], U16, name="par_list")
         x_w = held.tile([P, T], U32, name="x_w", align_bytes=64)
         x_s = held.tile([P, T], U8, name="x_s", align_bytes=64)
-        s1 = held.tile([P, E * H], U8, name="s1", align_bytes=64)
+        x_s_landing = shared.tile([P, T], U8, name="x_s_landing", tag="start", align_bytes=64)
+        s1 = held.tile([P, E // PLANES * H], U8, name="s1", align_bytes=64)
         sp = held.tile([P, E * H], U8, name="sp", align_bytes=64)
         s2 = held.tile([P, E // PLANES * N], U8, name="s2", align_bytes=64)
         ident = held.tile([P, P], F32, name="ident", align_bytes=64)
@@ -71,39 +71,43 @@ def tile_moe_duo_s_relu2_kernel(
                 dst = tile[start + r : P : QUADRANT, :].bitcast(I32).rearrange("q (e n) -> q e n", e=E)
                 nc.sync.dma_start(dst, rows[r].bitcast(I32))
 
-        def load_w2_scales(group):
+        def load_packed_scales(queue, tile, scales, group):
             for q in range(P // QUADRANT):
-                nc.sync.dma_start(
-                    s2[QUADRANT * q : QUADRANT * q + SCALE_ROWS * PLANES, group * N : (group + 1) * N].bitcast(I32),
-                    w2_scales[PLANES * group : PLANES * (group + 1), 0, SCALE_ROWS * q : SCALE_ROWS * (q + 1), :]
+                queue.dma_start(
+                    tile[QUADRANT * q : QUADRANT * q + SCALE_ROWS * PLANES, group * N : (group + 1) * N].bitcast(I32),
+                    scales[PLANES * group : PLANES * (group + 1), 0, SCALE_ROWS * q : SCALE_ROWS * (q + 1), :]
                     .bitcast(I32),
                 )
 
-        nc.gpsimd.memset(x_s[:].bitcast(I32), 0)
+        nc.gpsimd.memset(x_s_landing[:].bitcast(I32), 0)
         load_weights(nc.gpsimd, w1, w1_src, 0, 1, "w1")
         make_identity(nc, ident[:])
-        for tile in (sp, s1, s2):
+        for tile in (s1, sp, s2):
             nc.vector.memset(tile[:].bitcast(I32), 0)
+        load_packed_scales(nc.gpsimd, s1, w1_scales, 1)
         nc.sync.dma_start(tok_list[:], offs)
+        nc.sync.dma_start(x_w[:].bitcast(I32), x_words[0].rearrange("p n d -> p (n d)").bitcast(I32))
         nc.sync.dma_start(par_list[:], offs2)
         x_rows = x_scales[0].rearrange("(q r) n -> r q n", r=SCALE_ROWS)
         for r in range(SCALE_ROWS):
-            nc.sync.dma_start(x_s[r:P:QUADRANT, :].bitcast(I32), x_rows[r].bitcast(I32))
-        nc.sync.dma_start(x_w[:].bitcast(I32), x_words[0].rearrange("p n d -> p (n d)").bitcast(I32))
+            nc.sync.dma_start(x_s_landing[r:P:QUADRANT, :].bitcast(I32), x_rows[r].bitcast(I32))
         load_weights(nc.sync, wp, wp_src, 0, PAIR, "wp")
+        load_packed_scales(nc.sync, s1, w1_scales, 0)
         load_plane_rows(sp, 0, wp_scales)
-        load_plane_rows(s1, W1_PLANE_START, w1_scales)
-        load_weights(nc.sync, w1, w1_src, 1, PAIR, "w1")
+        load_weights(nc.sync, w1, w1_src, 1, 2, "w1")
         load_weights(nc.sync, w1, w1_src, 2, 3, "w1")
         load_weights(nc.sync, wp, wp_src, 2, 4, "wp")
-        load_w2_scales(0)
-        load_weights(nc.sync, w2, w2_src, *W2_LOADS[0], "w2")
+        load_packed_scales(nc.sync, s2, w2_scales, 0)
+        load_weights(nc.sync, w2, w2_src, 0, 2, "w2")
         load_weights(nc.sync, w1, w1_src, 3, 4, "w1")
-        load_first_layer(2 * PAIR)
-        load_weights(nc.sync, w2, w2_src, *W2_LOADS[1], "w2")
-        load_first_layer(3 * PAIR)
-        load_w2_scales(1)
-        load_weights(nc.sync, w2, w2_src, *W2_LOADS[2], "w2")
+        load_weights(nc.sync, w1, w1_src, 4, 5, "w1")
+        load_weights(nc.sync, wp, wp_src, 4, 6, "wp")
+        load_weights(nc.sync, w2, w2_src, 2, 3, "w2")
+        load_weights(nc.sync, w1, w1_src, 5, 6, "w1")
+        load_weights(nc.sync, w2, w2_src, 3, 5, "w2")
+        load_first_layer(6)
+        load_packed_scales(nc.sync, s2, w2_scales, 1)
+        load_weights(nc.sync, w2, w2_src, 5, 8, "w2")
 
         gathered, first, relu, squared, turned, hidden, codes, cscales = ({} for i in range(8))
 
@@ -115,74 +119,65 @@ def tile_moe_duo_s_relu2_kernel(
             offsets = (tok_list, par_list)[part % 2][:, first_col : first_col + cols]
             nc.vector.tensor_copy(dst, window[:].indirect(offsets))
 
-        def gather(n, tag):
-            e, part = divmod(n, 4)
-            tile = sbuf([P, C], U8 if part < 2 else U32, f"gathered{n}", tag)
-            gather_into(tile[:], part, e * LIST_COLS, LIST_COLS)
-            for a in range(HALVES):
-                gathered[e, a, part] = tile[:, a * P : (a + 1) * P]
-
-        def gather_half(a, sort, tag):
-            tile = sbuf([P, 2, P], U32 if sort else U8, f"gathered_half{a}_{sort}", tag)
+        def gather(e, sort, tile):
             for j in range(2):
-                gathered[E - 1, a, 2 * sort + j] = tile[:, j, :]
-                gather_into(tile[:, j, :], 2 * sort + j, (E - 1) * LIST_COLS + a * P // 16, P // 16)
+                gather_into(tile[:, j, :], 2 * sort + j, e * LIST_COLS, LIST_COLS)
+                for a in range(HALVES):
+                    gathered[e, a, 2 * sort + j] = tile[:, j, a * P : (a + 1) * P]
 
-        def hand(k, j):
-            return f"after{k - 1}" if j == 2 else f"hand{k}_{j}"
+        def gather_bytes(e, tag):
+            gather(e, 0, sbuf([P, 2, C], U8, f"bytes{e}", tag))
 
-        held_order = [12, 13] + list(range(16, 4 * E))
+        def gather_words(e, tag):
+            gather(e, 1, sbuf([P, 2, C], U32, f"words{e}", tag))
 
-        def held_gather(k, j):
-            if j < GROUPS[k]:
-                gather(held_order[sum(GROUPS[:k]) + j], hand(k, j))
-            elif k == len(GROUPS) - 1 and j < 3:
-                gather_half(0, j - 1, hand(k, j))
+        S, V = "scalar", "vector"
 
         def bank(shape, name, tag):
             return psum.tile(shape, F32, name=name, tag=tag)
 
-        def first_layer(e, a, tag):
-            cols = slice(e * H, (e + 1) * H)
-            tok_s, par_s, tok, par = (gathered[e, a, part] for part in range(4))
+        def token_product(e, a, tag):
             first[e, a] = bank([P, H], f"first{e}_{a}", tag)
             nc.tensor.matmul_mx(
-                out=first[e, a][:], lhsT=tok.bitcast(FP8X4), lhsT_scale=tok_s,
-                rhs=w1[e].bitcast(FP8X4), rhs_scale=s1[W1_PLANE_START:P, cols], start=True, stop=False,
+                out=first[e, a][:], lhsT=gathered[e, a, 2].bitcast(FP8X4), lhsT_scale=gathered[e, a, 0],
+                rhs=w1[e].bitcast(FP8X4),
+                rhs_scale=s1[SCALE_ROWS * (e % PLANES) : P, e // PLANES * H : (e // PLANES + 1) * H],
+                start=True, stop=False,
             )
+
+        def partner_product(e, a):
             nc.tensor.matmul_mx(
-                out=first[e, a][:], lhsT=par.bitcast(FP8X4), lhsT_scale=par_s,
-                rhs=wp[e].bitcast(FP4X4), rhs_scale=sp[:, cols], start=False, stop=True,
+                out=first[e, a][:], lhsT=gathered[e, a, 3].bitcast(FP8X4), lhsT_scale=gathered[e, a, 1],
+                rhs=wp[e].bitcast(FP4X4), rhs_scale=sp[:, e * H : (e + 1) * H], start=False, stop=True,
             )
+
+        def first_layer(e, a, tag):
+            token_product(e, a, tag)
+            partner_product(e, a)
 
         def paired(e, a):
             return a == 0 and e < PAIRED_EXPERTS
 
-        def relu_tag(e, a):
-            if e == E - 2:
-                return f"hand{e - 2}_4" if a == 0 else f"hand{e - 1}_1"
-            return f"hand{e - 1}_1" if a else f"hand{e - 2}_4"
-
-        def rectify(e, a):
-            relu[e, a] = sbuf([P, H], F32, f"relu{e}_{a}", relu_tag(e, a))
+        def rectify(e, a, engine=None, tag=None):
+            relu[e, a] = sbuf([P, H], F32, f"relu{e}_{a}", tag or f"relu{e}_{a}")
             if paired(e, a):
                 dst = relu[e, a][:].rearrange("s (u p d) -> s u p d", u=2, d=2)
                 src = first[e, a][:].rearrange("s (p u d) -> s u p d", u=2, d=2)
             else:
                 dst = relu[e, a][:].rearrange("s (t p) -> s t p", t=PACK)
                 src = first[e, a][:].rearrange("s (p t) -> s t p", t=PACK)
-            if e == E - 1 or (e, a) == (E - 2, 0):
+            if engine == V:
                 nc.vector.tensor_scalar(dst, src, 0.0, None, MAX)
             else:
                 nc.scalar.activation(dst, src, ACT.Relu)
 
         def square_pairs(e):
-            squared[e] = sbuf([P, H], BF16, f"squared{e}", f"after{e - 2}")
+            squared[e] = sbuf([P, H], BF16, f"squared{e}", f"squared{e}")
             nc.gpsimd.tensor_tensor(squared[e][:], relu[e, 0][:], relu[e, 0][:], MULT)
 
         def hidden_tile(e, a):
-            hidden[e, a] = sbuf([P, P * PACK], BF16, f"hidden{e}_{a}", f"hand{e}_0" if a else f"after{e}")
-            return hidden[e, a]
+            hidden[e, a] = sbuf([P, P * PACK], BF16, f"hidden{e}_{a}", f"hidden{e}_{a}")
+            return hidden[e, a][:]
 
         def turn_pairs(e, tag):
             turned[e, 0] = bank([P, 2, P], f"turned{e}_0", tag)
@@ -191,7 +186,7 @@ def tile_moe_duo_s_relu2_kernel(
                 nc.tensor.transpose(turned[e, 0][:, u, :], pairs[:, u * P : (u + 1) * P], ident[:])
 
         def copy_pairs(e, copy):
-            dst = hidden_tile(e, 0)[:].bitcast(F32).rearrange("p (s u) -> p s u", u=2)
+            dst = hidden_tile(e, 0).bitcast(F32).rearrange("p (s u) -> p s u", u=2)
             copy(dst, turned[e, 0][:].rearrange("p u s -> p s u"))
 
         def turn_values(e, a, tag):
@@ -200,64 +195,77 @@ def tile_moe_duo_s_relu2_kernel(
                 nc.tensor.transpose(turned[e, a][:, t, :], relu[e, a][:, t * P : (t + 1) * P], ident[:])
 
         def square_values(e, a):
-            dst = hidden_tile(e, a)[:].rearrange("p (s t) -> p s t", t=PACK)
+            dst = hidden_tile(e, a).rearrange("p (s t) -> p s t", t=PACK)
             nc.scalar.activation(dst, turned[e, a][:].rearrange("p t s -> p s t"), ACT.Square)
 
-        def quantize(e):
-            codes[e] = sbuf([P, C], U32, f"codes{e}", f"hand{e}_3")
+        def new_codes(e):
+            codes[e] = held.tile([P, C], U32, name=f"codes{e}", align_bytes=64)
             cscales[e] = held.tile([P, C], U8, name=f"cscales{e}", align_bytes=64)
-            for a in range(HALVES):
-                cols = slice(a * P, (a + 1) * P)
-                nc.vector.quantize_mx(out=codes[e][:, cols].bitcast(FP8X4), scales=cscales[e][:, cols], in_=hidden[e, a][:])
+
+        def quantize_half(e, a):
+            cols = slice(a * P, (a + 1) * P)
+            nc.vector.quantize_mx(out=codes[e][:, cols].bitcast(FP8X4), scales=cscales[e][:, cols], in_=hidden[e, a][:])
+
+        def quantize(e):
+            new_codes(e)
+            for a in (1, 0):
+                quantize_half(e, a)
+
+        def output_block(result, e, block, slots):
+            n0 = block * P
+            col = e // PLANES * N + n0
+            nc.tensor.matmul_mx(
+                out=result, lhsT=w2[e][:, PACK * n0 : PACK * (n0 + P)].bitcast(FP8X4),
+                lhsT_scale=s2[SCALE_ROWS * (e % PLANES) : P, col : col + P],
+                rhs=codes[e][:, slots].bitcast(FP8X4), rhs_scale=cscales[e][:, slots], start=True, stop=True,
+            )
+
+        def finish_half(e, a, block, blocks, tag, copy):
+            result = bank([P, blocks, P], f"result{e}_{a}_{block}", tag)
+            for j in range(blocks):
+                output_block(result[:, j, :], e, block + j, slice(a * P, (a + 1) * P))
+            staged = held.tile([P, blocks, P], F32, name=f"staged{e}_{a}_{block}", align_bytes=64)
+            copy(staged[:], result[:])
+            rows = out[block * P : (block + blocks) * P, e * C + a * P : e * C + (a + 1) * P]
+            nc.sync.dma_start(rows.rearrange("(j p) c -> p j c", p=P), staged[:])
 
         def second_layer(e, part, tag):
             result = bank([P, 2, C], f"result{e}_{part}", tag)
             for j in range(2):
-                n0 = (2 * part + j) * P
-                col = e // PLANES * N + n0
-                nc.tensor.matmul_mx(
-                    out=result[:, j, :], lhsT=w2[e][:, PACK * n0 : PACK * (n0 + P)].bitcast(FP8X4),
-                    lhsT_scale=s2[SCALE_ROWS * (e % PLANES) : P, col : col + P],
-                    rhs=codes[e][:].bitcast(FP8X4), rhs_scale=cscales[e][:], start=True, stop=True,
-                )
+                output_block(result[:, j, :], e, 2 * part + j, slice(0, C))
             return result
 
-        def store(e, part, result, copy):
-            staged = held.tile([P, 2, C], F32, name=f"staged{e}_{part}", align_bytes=64)
+        def store(e, part, result, copy, tag=None):
+            staged = sbuf([P, 2, C], F32, f"staged{e}_{part}", tag or f"staged{e}_{part}")
             copy(staged[:], result[:])
             rows = out[2 * part * P : (2 * part + 2) * P, e * C : (e + 1) * C]
             nc.sync.dma_start(rows.rearrange("(j p) c -> p j c", p=P), staged[:])
 
-        for n in range(8):
-            gather(n, f"free{n}")
-        for n in (10, 11):
-            gather(n, f"free{n}")
+        gather_words(0, "words0")
+        nc.vector.tensor_copy(x_s[:].bitcast(I32), x_s_landing[:].bitcast(I32))
+        early_words = sbuf([P, 6, C], U32, "early_words", "start")
+        for e in range(3):
+            gather_bytes(e, f"bytes{e}")
+            gather(e + 1, 1, early_words[:, 2 * e : 2 * e + 2, :])
         for e in range(E - 2):
             k = e - 2
             for a in range(HALVES):
                 first_layer(e, a, f"result1_{a}" if e == 0 else f"first{a}")
                 rectify(e, a)
-            if e == 0:
-                for n, giver in ((8, 0), (9, 2), (14, 1), (15, 3)):
-                    gather(n, f"free{giver}")
             if k >= 0:
                 quantize(k)
+                gather_bytes(k + 3, f"hidden{k}_1")
+                gather_words(k + 4, f"hidden{k}_0")
             square_pairs(e)
             if e >= 1:
                 turn_values(e - 1, 1, "turned1")
                 turn_pairs(e - 1, "turned0")
-            if k >= 0:
-                for j in range(3):
-                    held_gather(k, j)
-            if e >= 1:
                 square_values(e - 1, 1)
                 copy_pairs(e - 1, nc.scalar.copy)
             if k >= 0:
                 banks = [second_layer(k, part, f"result{k % 2}_{part}") for part in range(2)]
-                held_gather(k, 3)
-                held_gather(k, 4)
-                store(k, 0, banks[0], nc.scalar.copy)
-                store(k, 1, banks[1], nc.scalar.copy)
+                for part in range(2):
+                    store(k, part, banks[part], nc.scalar.copy)
 
         def finish(e, part, tag, copy):
             store(e, part, second_layer(e, part, tag), copy)
@@ -266,36 +274,42 @@ def tile_moe_duo_s_relu2_kernel(
         last = E - 1
         for a in range(HALVES):
             first_layer(last - 1, a, f"first{a}")
-        rectify(last - 1, 0)
+            rectify(last - 1, a)
         quantize(last - 3)
+        gather_bytes(last, f"hidden{last - 3}_1")
+        square_pairs(last - 1)
         turn_values(last - 2, 1, "turned1")
         turn_pairs(last - 2, "turned0")
-        for sort in range(2):
-            gather_half(1, sort, hand(last - 3, sort))
-        square_pairs(last - 1)
-        first_layer(last, 0, "result1_0")
         square_values(last - 2, 1)
         copy_pairs(last - 2, on_scalar)
-        rectify(last - 1, 1)
-        for part in range(2):
-            finish(last - 3, part, f"result0_{part}", on_scalar)
-        first_layer(last, 1, "result1_1")
-        rectify(last, 0)
-        quantize(last - 2)
-        rectify(last, 1)
+        banks = [second_layer(last - 3, part, f"result0_{part}") for part in range(2)]
+        for a in range(HALVES):
+            token_product(last, a, f"result1_{a}")
+        for a in range(HALVES):
+            partner_product(last, a)
+        store(last - 3, 0, banks[0], on_vector)
+        store(last - 3, 1, banks[1], on_scalar)
         turn_values(last - 1, 1, "turned1")
-        turn_values(last, 0, "first0")
         turn_pairs(last - 1, "turned0")
-        turn_values(last, 1, "first1")
+        quantize(last - 2)
+        rectify(last, 0, V, f"hidden{last - 2}_1")
+        rectify(last, 1, S)
+        banks = [second_layer(last - 2, part, f"result0_{part}") for part in range(2)]
+        for a in range(HALVES):
+            turn_values(last, a, f"first{a}")
         square_values(last - 1, 1)
         copy_pairs(last - 1, on_vector)
-        finish(last - 2, 0, "result0_0", on_vector)
         quantize(last - 1)
-        finish(last - 2, 1, "result0_1", on_vector)
+        store(last - 2, 0, banks[0], on_scalar)
+        store(last - 2, 1, banks[1], on_vector, f"hidden{last - 1}_1")
+        banks = [second_layer(last - 1, part, f"result1_{part}") for part in range(2)]
         for a in range(HALVES):
             square_values(last, a)
-        quantize(last)
-        finish(last - 1, 0, "result1_0", on_vector)
-        finish(last - 1, 1, "result1_1", on_scalar)
-        finish(last, 0, "turned0", on_vector)
-        finish(last, 1, "turned1", on_scalar)
+        new_codes(last)
+        quantize_half(last, 0)
+        store(last - 1, 0, banks[0], on_vector, f"hidden{last}_0")
+        quantize_half(last, 1)
+        store(last - 1, 1, banks[1], on_scalar)
+        finish_half(last, 0, 0, 4, "turned0", on_scalar)
+        finish_half(last, 1, 0, 2, "turned1", on_vector)
+        finish_half(last, 1, 2, 2, "result0_0", on_scalar)

@@ -28,6 +28,7 @@ PAIR = 2
 W2_LOADS = [(0, 2), (2, 5), (5, 8)]
 MULT = mybir.AluOpType.mult
 MAX = mybir.AluOpType.max
+PAIRED_STORES = 4
 PAIRED_EXPERTS = E - 1
 
 
@@ -91,23 +92,20 @@ def tile_moe_duo_s_relu2_kernel(
         x_rows = x_scales[0].rearrange("(q r) n -> r q n", r=SCALE_ROWS)
         for r in range(SCALE_ROWS):
             nc.sync.dma_start(x_s_landing[r:P:QUADRANT, :].bitcast(I32), x_rows[r].bitcast(I32))
-        load_weights(nc.sync, wp, wp_src, 0, PAIR, "wp")
+        load_weights(nc.sync, wp, wp_src, 0, 4, "wp")
         load_packed_scales(nc.sync, s1, w1_scales, 0)
         load_plane_rows(sp, 0, wp_scales)
-        load_weights(nc.sync, w1, w1_src, 1, 2, "w1")
-        load_weights(nc.sync, w1, w1_src, 2, 3, "w1")
-        load_weights(nc.sync, wp, wp_src, 2, 4, "wp")
+        load_weights(nc.sync, w1, w1_src, 1, 3, "w1")
         load_packed_scales(nc.sync, s2, w2_scales, 0)
         load_weights(nc.sync, w2, w2_src, 0, 2, "w2")
-        load_weights(nc.sync, w1, w1_src, 3, 4, "w1")
-        load_weights(nc.sync, w1, w1_src, 4, 5, "w1")
-        load_weights(nc.sync, wp, wp_src, 4, 6, "wp")
-        load_weights(nc.sync, w2, w2_src, 2, 3, "w2")
-        load_weights(nc.sync, w1, w1_src, 5, 6, "w1")
-        load_weights(nc.sync, w2, w2_src, 3, 5, "w2")
-        load_first_layer(6)
+        load_weights(nc.sync, w1, w1_src, 3, 5, "w1")
+        load_weights(nc.sync, wp, wp_src, 4, 8, "wp")
+        load_weights(nc.sync, w2, w2_src, 2, 4, "w2")
+        load_weights(nc.sync, w1, w1_src, 5, 7, "w1")
         load_packed_scales(nc.sync, s2, w2_scales, 1)
-        load_weights(nc.sync, w2, w2_src, 5, 8, "w2")
+        load_weights(nc.sync, w2, w2_src, 4, 6, "w2")
+        load_weights(nc.sync, w1, w1_src, 7, 8, "w1")
+        load_weights(nc.sync, w2, w2_src, 6, 8, "w2")
 
         gathered, first, relu, squared, turned, hidden, codes, cscales = ({} for i in range(8))
 
@@ -224,10 +222,10 @@ def tile_moe_duo_s_relu2_kernel(
             result = bank([P, blocks, P], f"result{e}_{a}_{block}", tag)
             for j in range(blocks):
                 output_block(result[:, j, :], e, block + j, slice(a * P, (a + 1) * P))
-            staged = held.tile([P, blocks, P], F32, name=f"staged{e}_{a}_{block}", align_bytes=64)
-            copy(staged[:], result[:])
+            tile = held.tile([P, blocks, P], F32, name=f"staged{e}_{a}_{block}", align_bytes=64)
+            copy(tile[:], result[:])
             rows = out[block * P : (block + blocks) * P, e * C + a * P : e * C + (a + 1) * P]
-            nc.sync.dma_start(rows.rearrange("(j p) c -> p j c", p=P), staged[:])
+            nc.sync.dma_start(rows.rearrange("(j p) c -> p j c", p=P), tile[:])
 
         def second_layer(e, part, tag):
             result = bank([P, 2, C], f"result{e}_{part}", tag)
@@ -236,11 +234,17 @@ def tile_moe_duo_s_relu2_kernel(
             return result
 
         def store(e, part, result, copy, tag=None):
-            staged = sbuf([P, 2, C], F32, f"staged{e}_{part}", tag or f"staged{e}_{part}")
-            copy(staged[:], result[:])
-            rows = out[2 * part * P : (2 * part + 2) * P, e * C : (e + 1) * C]
-            nc.sync.dma_start(rows.rearrange("(j p) c -> p j c", p=P), staged[:])
+            width = 2 if e < PAIRED_STORES else 1
+            first_e = e - e % width
+            if (first_e, part) not in staged:
+                staged[first_e, part] = sbuf([P, 2, width * C], F32, f"staged{e}_{part}", tag or f"staged{e}_{part}")
+            tile = staged[first_e, part]
+            copy(tile[:, :, (e - first_e) * C : (e - first_e + 1) * C], result[:])
+            if e == first_e + width - 1:
+                rows = out[2 * part * P : (2 * part + 2) * P, first_e * C : (e + 1) * C]
+                nc.sync.dma_start(rows.rearrange("(j p) c -> p j c", p=P), tile[:])
 
+        staged = {}
         gather_words(0, "words0")
         nc.vector.tensor_copy(x_s[:].bitcast(I32), x_s_landing[:].bitcast(I32))
         early_words = sbuf([P, 6, C], U32, "early_words", "start")

@@ -72,8 +72,8 @@ def tile_moe_duo_s_relu2_kernel(
                 dst = tile[start + r : P : QUADRANT, :].bitcast(I32).rearrange("q (e n) -> q e n", e=E)
                 nc.sync.dma_start(dst, rows[r].bitcast(I32))
 
-        def load_packed_scales(queue, tile, scales, group):
-            for q in range(P // QUADRANT):
+        def load_packed_scales(queue, tile, scales, group, quadrants=range(P // QUADRANT)):
+            for q in quadrants:
                 queue.dma_start(
                     tile[QUADRANT * q : QUADRANT * q + SCALE_ROWS * PLANES, group * N : (group + 1) * N].bitcast(I32),
                     scales[PLANES * group : PLANES * (group + 1), 0, SCALE_ROWS * q : SCALE_ROWS * (q + 1), :]
@@ -81,7 +81,6 @@ def tile_moe_duo_s_relu2_kernel(
                 )
 
         nc.gpsimd.memset(x_s_landing[:].bitcast(I32), 0)
-        load_weights(nc.gpsimd, w1, w1_src, 0, 1, "w1")
         make_identity(nc, ident[:])
         for tile in (s1, sp, s2):
             nc.vector.memset(tile[:].bitcast(I32), 0)
@@ -92,19 +91,22 @@ def tile_moe_duo_s_relu2_kernel(
         x_rows = x_scales[0].rearrange("(q r) n -> r q n", r=SCALE_ROWS)
         for r in range(SCALE_ROWS):
             nc.sync.dma_start(x_s_landing[r:P:QUADRANT, :].bitcast(I32), x_rows[r].bitcast(I32))
-        load_weights(nc.sync, wp, wp_src, 0, 4, "wp")
-        load_packed_scales(nc.sync, s1, w1_scales, 0)
+        load_packed_scales(nc.sync, s1, w1_scales, 0, range(0, 1))
+        load_weights(nc.sync, w1, w1_src, 0, 1, "w1")
+        load_weights(nc.sync, wp, wp_src, 0, 2, "wp")
+        load_packed_scales(nc.sync, s1, w1_scales, 0, range(1, 4))
         load_plane_rows(sp, 0, wp_scales)
         load_weights(nc.sync, w1, w1_src, 1, 3, "w1")
+        load_weights(nc.sync, wp, wp_src, 2, 4, "wp")
         load_packed_scales(nc.sync, s2, w2_scales, 0)
         load_weights(nc.sync, w2, w2_src, 0, 2, "w2")
-        load_weights(nc.sync, w1, w1_src, 3, 5, "w1")
+        load_weights(nc.sync, w1, w1_src, 3, 4, "w1")
         load_weights(nc.sync, wp, wp_src, 4, 8, "wp")
+        load_weights(nc.sync, w1, w1_src, 4, 6, "w1")
         load_weights(nc.sync, w2, w2_src, 2, 4, "w2")
-        load_weights(nc.sync, w1, w1_src, 5, 7, "w1")
+        load_weights(nc.sync, w1, w1_src, 6, 8, "w1")
         load_packed_scales(nc.sync, s2, w2_scales, 1)
         load_weights(nc.sync, w2, w2_src, 4, 6, "w2")
-        load_weights(nc.sync, w1, w1_src, 7, 8, "w1")
         load_weights(nc.sync, w2, w2_src, 6, 8, "w2")
 
         gathered, first, relu, squared, turned, hidden, codes, cscales = ({} for i in range(8))

@@ -28,7 +28,7 @@ PAIR = 2
 W2_LOADS = [(0, 2), (2, 5), (5, 8)]
 MULT = mybir.AluOpType.mult
 MAX = mybir.AluOpType.max
-PAIRED_STORES = 4
+PAIRED_STORES = 2
 PAIRED_EXPERTS = E - 1
 
 
@@ -220,14 +220,12 @@ def tile_moe_duo_s_relu2_kernel(
                 rhs=codes[e][:, slots].bitcast(FP8X4), rhs_scale=cscales[e][:, slots], start=True, stop=True,
             )
 
-        def finish_half(e, a, block, blocks, tag, copy):
-            result = bank([P, blocks, P], f"result{e}_{a}_{block}", tag)
-            for j in range(blocks):
-                output_block(result[:, j, :], e, block + j, slice(a * P, (a + 1) * P))
-            tile = held.tile([P, blocks, P], F32, name=f"staged{e}_{a}_{block}", align_bytes=64)
+        def finish_block(e, block, tag, copy):
+            result = bank([P, C], f"result{e}_block{block}", tag)
+            output_block(result[:], e, block, slice(0, C))
+            tile = held.tile([P, C], F32, name=f"staged{e}_block{block}", align_bytes=64)
             copy(tile[:], result[:])
-            rows = out[block * P : (block + blocks) * P, e * C + a * P : e * C + (a + 1) * P]
-            nc.sync.dma_start(rows.rearrange("(j p) c -> p j c", p=P), tile[:])
+            nc.sync.dma_start(out[block * P : (block + 1) * P, e * C : (e + 1) * C], tile[:])
 
         def second_layer(e, part, tag):
             result = bank([P, 2, C], f"result{e}_{part}", tag)
@@ -311,11 +309,8 @@ def tile_moe_duo_s_relu2_kernel(
         banks = [second_layer(last - 1, part, f"result1_{part}") for part in range(2)]
         for a in range(HALVES):
             square_values(last, a)
-        new_codes(last)
-        quantize_half(last, 0)
-        store(last - 1, 0, banks[0], on_vector, f"hidden{last}_0")
-        quantize_half(last, 1)
+        store(last - 1, 0, banks[0], on_vector)
+        quantize(last)
         store(last - 1, 1, banks[1], on_scalar)
-        finish_half(last, 0, 0, 4, "turned0", on_scalar)
-        finish_half(last, 1, 0, 2, "turned1", on_vector)
-        finish_half(last, 1, 2, 2, "result0_0", on_scalar)
+        for block, tag in enumerate(("turned0", "turned1", "result0_0", "result0_1")):
+            finish_block(last, block, tag, on_scalar if block % 2 else on_vector)

@@ -28,7 +28,7 @@ PAIR = 2
 W2_LOADS = [(0, 2), (2, 5), (5, 8)]
 MULT = mybir.AluOpType.mult
 MAX = mybir.AluOpType.max
-PAIRED_STORES = 2
+PAIRED_STORES = 4
 PAIRED_EXPERTS = E - 1
 
 
@@ -106,8 +106,7 @@ def tile_moe_duo_s_relu2_kernel(
         load_weights(nc.sync, w2, w2_src, 2, 4, "w2")
         load_weights(nc.sync, w1, w1_src, 6, 8, "w1")
         load_packed_scales(nc.sync, s2, w2_scales, 1)
-        load_weights(nc.sync, w2, w2_src, 4, 6, "w2")
-        load_weights(nc.sync, w2, w2_src, 6, 8, "w2")
+        load_weights(nc.sync, w2, w2_src, 4, 8, "w2")
 
         gathered, first, relu, squared, turned, hidden, codes, cscales = ({} for i in range(8))
 

@@ -114,7 +114,7 @@ def tile_moe_duo_s_relu2_kernel(
             return shared.tile(shape, dtype, name=name, tag=tag, align_bytes=64)
 
         def gather_into(dst, part, first_col, cols):
-            window = x_s if part < 2 else x_w
+            window = x_w if part >= 2 else x_s_landing if (part, first_col) == (0, 0) else x_s
             offsets = (tok_list, par_list)[part % 2][:, first_col : first_col + cols]
             nc.vector.tensor_copy(dst, window[:].indirect(offsets))
 

@@ -29,6 +29,8 @@ W2_LOADS = [(0, 2), (2, 5), (5, 8)]
 MULT = mybir.AluOpType.mult
 MAX = mybir.AluOpType.max
 PAIRED_STORES = 4
+LAID_EXPERTS = 4
+LAID_BYTES = 2 * C + 2 * C * 4
 PAIRED_EXPERTS = E - 1
 
 
@@ -39,6 +41,7 @@ def tile_moe_duo_s_relu2_kernel(
     with ExitStack() as ctx:
         held = ctx.enter_context(tc.tile_pool(name="held", bufs=1))
         shared = ctx.enter_context(tc.tile_pool(name="shared", bufs=1))
+        laid = ctx.enter_context(tc.tile_pool(name="laid", bufs=1))
         psum = ctx.enter_context(tc.psum_pool(name="psum", bufs=1))
 
         tok_list = held.tile([P, E * LIST_COLS], U16, name="tok_list")
@@ -113,6 +116,9 @@ def tile_moe_duo_s_relu2_kernel(
         def sbuf(shape, dtype, name, tag):
             return shared.tile(shape, dtype, name=name, tag=tag, align_bytes=64)
 
+        def laid_tile(shape, dtype, name, offset):
+            return laid.tile(shape, dtype, name=name, align_bytes=64, offset=offset)
+
         def gather_into(dst, part, first_col, cols):
             window = x_w if part >= 2 else x_s_landing if (part, first_col) == (0, 0) else x_s
             offsets = (tok_list, par_list)[part % 2][:, first_col : first_col + cols]
@@ -171,11 +177,14 @@ def tile_moe_duo_s_relu2_kernel(
                 nc.scalar.activation(dst, src, ACT.Relu)
 
         def square_pairs(e):
-            squared[e] = sbuf([P, H], BF16, f"squared{e}", f"squared{e}")
+            squared[e] = sbuf([P, H], BF16, f"squared{e}", f"hidden{e - 2}_0" if e >= 2 else f"squared{e}")
             nc.gpsimd.tensor_tensor(squared[e][:], relu[e, 0][:], relu[e, 0][:], MULT)
 
         def hidden_tile(e, a):
-            hidden[e, a] = sbuf([P, P * PACK], BF16, f"hidden{e}_{a}", f"hidden{e}_{a}")
+            if a == 1 and e < LAID_EXPERTS:
+                hidden[e, a] = laid_tile([P, P * PACK], BF16, f"hidden{e}_{a}", e * LAID_BYTES)
+            else:
+                hidden[e, a] = sbuf([P, P * PACK], BF16, f"hidden{e}_{a}", f"hidden{e}_{a}")
             return hidden[e, a][:]
 
         def turn_pairs(e, tag):
@@ -257,8 +266,8 @@ def tile_moe_duo_s_relu2_kernel(
                 rectify(e, a)
             if k >= 0:
                 quantize(k)
-                gather_bytes(k + 3, f"hidden{k}_1")
-                gather_words(k + 4, f"hidden{k}_0")
+                gather(k + 3, 0, laid_tile([P, 2, C], U8, f"bytes{k + 3}", k * LAID_BYTES))
+                gather(k + 4, 1, laid_tile([P, 2, C], U32, f"words{k + 4}", k * LAID_BYTES + 2 * C))
             square_pairs(e)
             if e >= 1:
                 turn_values(e - 1, 1, "turned1")

from contextlib import ExitStack

import concourse.mybir as mybir
from concourse.masks import make_identity

K, T, E, C, H, N = 512, 512, 8, 256, 512, 512
FLOPS = 2 * E * C * (2 * K * H + H * N)

F32 = mybir.dt.float32
BF16 = mybir.dt.bfloat16
I32 = mybir.dt.int32
U32 = mybir.dt.uint32
U16 = mybir.dt.uint16
U8 = mybir.dt.uint8
FP8X4 = mybir.dt.float8_e4m3fn_x4
FP4X4 = mybir.dt.float4_e2m1fn_x4
ACT = mybir.ActivationFunctionType

P = 128
PACK = 4
HALVES = C // P
LIST_COLS = C // 16
QUADRANT = 32
SCALE_ROWS = 4
PLANES = 4
W1_PLANE_START = 4
PAIR = 2
W2_LOADS = [(0, 2), (2, 5), (5, 8)]
MULT = mybir.AluOpType.mult
MAX = mybir.AluOpType.max
PAIRED_STORES = 4
LAID_EXPERTS = 4
LAID_BYTES = 2 * C + 2 * C * 4
PAIRED_EXPERTS = E - 1


def tile_moe_duo_s_relu2_kernel(
    tc, x_words, x_scales, w1_words, w1_scales, wp_words, wp_scales, w2_words, w2_scales, offs, offs2, out
):
    nc = tc.nc
    with ExitStack() as ctx:
        held = ctx.enter_context(tc.tile_pool(name="held", bufs=1))
        shared = ctx.enter_context(tc.tile_pool(name="shared", bufs=1))
        laid = ctx.enter_context(tc.tile_pool(name="laid", bufs=1))
        psum = ctx.enter_context(tc.psum_pool(name="psum", bufs=1))

        tok_list = held.tile([P, E * LIST_COLS], U16, name="tok_list")
        par_list = held.tile([P, E * LIST_COLS], U16, name="par_list")
        x_w = held.tile([P, T], U32, name="x_w", align_bytes=64)
        x_s = held.tile([P, T], U8, name="x_s", align_bytes=64)
        x_s_landing = shared.tile([P, T], U8, name="x_s_landing", tag="start", align_bytes=64)
        s1 = held.tile([P, E // PLANES * H], U8, name="s1", align_bytes=64)
        sp = held.tile([P, E * H], U8, name="sp", align_bytes=64)
        s2 = held.tile([P, E // PLANES * N], U8, name="s2", align_bytes=64)
        ident = held.tile([P, P], F32, name="ident", align_bytes=64)
        w1, wp, w2 = {}, {}, {}

        w1_src = w1_words.rearrange("e s p n d -> e (s p) (n d)").bitcast(I32)
        wp_src = wp_words.rearrange("e s p n -> e (s p) n").bitcast(I32)
        w2_src = w2_words.rearrange("e s p n d -> e (s p) (n d)").bitcast(I32)

        def load_weights(queue, store, src, first, last, name):
            tile = held.tile([P, last - first, 4 * src.shape[-1]], U8, name=f"{name}_{first}", align_bytes=64)
            queue.dma_start(tile[:].bitcast(I32), src[first:last].rearrange("e p n -> p e n"))
            for e in range(first, last):
                store[e] = tile[:, e - first, :]

        def load_first_layer(first):
            load_weights(nc.sync, w1, w1_src, first, first + PAIR, "w1")
            load_weights(nc.sync, wp, wp_src, first, first + PAIR, "wp")

        def load_plane_rows(tile, start, scales):
            rows = scales.rearrange("e s (q r) n -> r q (e s) n", r=SCALE_ROWS)
            for r in range(SCALE_ROWS):
                dst = tile[start + r : P : QUADRANT, :].bitcast(I32).rearrange("q (e n) -> q e n", e=E)
                nc.sync.dma_start(dst, rows[r].bitcast(I32))

        def load_packed_scales(queue, tile, scales, group, quadrants=range(P // QUADRANT)):
            for q in quadrants:
                queue.dma_start(
                    tile[QUADRANT * q : QUADRANT * q + SCALE_ROWS * PLANES, group * N : (group + 1) * N].bitcast(I32),
                    scales[PLANES * group : PLANES * (group + 1), 0, SCALE_ROWS * q : SCALE_ROWS * (q + 1), :]
                    .bitcast(I32),
                )

        nc.gpsimd.memset(x_s_landing[:].bitcast(I32), 0)
        make_identity(nc, ident[:])
        for tile in (s1, sp, s2):
            nc.vector.memset(tile[:].bitcast(I32), 0)
        load_packed_scales(nc.gpsimd, s1, w1_scales, 1)
        nc.sync.dma_start(tok_list[:], offs)
        nc.sync.dma_start(x_w[:].bitcast(I32), x_words[0].rearrange("p n d -> p (n d)").bitcast(I32))
        nc.sync.dma_start(par_list[:], offs2)
        x_rows = x_scales[0].rearrange("(q r) n -> r q n", r=SCALE_ROWS)
        for r in range(SCALE_ROWS):
            nc.sync.dma_start(x_s_landing[r:P:QUADRANT, :].bitcast(I32), x_rows[r].bitcast(I32))
        load_packed_scales(nc.sync, s1, w1_scales, 0, range(0, 1))
        load_weights(nc.sync, w1, w1_src, 0, 1, "w1")
        load_weights(nc.sync, wp, wp_src, 0, 2, "wp")
        load_packed_scales(nc.sync, s1, w1_scales, 0, range(1, 4))
        load_plane_rows(sp, 0, wp_scales)
        load_weights(nc.sync, w1, w1_src, 1, 3, "w1")
        load_weights(nc.sync, wp, wp_src, 2, 4, "wp")
        load_packed_scales(nc.sync, s2, w2_scales, 0)
        load_weights(nc.sync, w2, w2_src, 0, 2, "w2")
        load_weights(nc.sync, w1, w1_src, 3, 4, "w1")
        load_weights(nc.sync, wp, wp_src, 4, 8, "wp")
        load_weights(nc.sync, w1, w1_src, 4, 6, "w1")
        load_weights(nc.sync, w2, w2_src, 2, 4, "w2")
        load_weights(nc.sync, w1, w1_src, 6, 8, "w1")
        load_packed_scales(nc.sync, s2, w2_scales, 1)
        load_weights(nc.sync, w2, w2_src, 4, 8, "w2")

        gathered, first, relu, squared, turned, hidden, codes, cscales = ({} for i in range(8))

        def sbuf(shape, dtype, name, tag):
            return shared.tile(shape, dtype, name=name, tag=tag, align_bytes=64)

        def laid_tile(shape, dtype, name, offset):
            return laid.tile(shape, dtype, name=name, align_bytes=64, offset=offset)

        def gather_into(dst, part, first_col, cols):
            window = x_w if part >= 2 else x_s_landing if (part, first_col) == (0, 0) else x_s
            offsets = (tok_list, par_list)[part % 2][:, first_col : first_col + cols]
            nc.vector.tensor_copy(dst, window[:].indirect(offsets))

        def gather(e, sort, tile):
            for j in range(2):
                gather_into(tile[:, j, :], 2 * sort + j, e * LIST_COLS, LIST_COLS)
                for a in range(HALVES):
                    gathered[e, a, 2 * sort + j] = tile[:, j, a * P : (a + 1) * P]

        def gather_bytes(e, tag):
            gather(e, 0, sbuf([P, 2, C], U8, f"bytes{e}", tag))

        def gather_words(e, tag):
            gather(e, 1, sbuf([P, 2, C], U32, f"words{e}", tag))

        S, V = "scalar", "vector"

        def bank(shape, name, tag):
            return psum.tile(shape, F32, name=name, tag=tag)

        def token_product(e, a, tag):
            first[e, a] = bank([P, H], f"first{e}_{a}", tag)
            nc.tensor.matmul_mx(
                out=first[e, a][:], lhsT=gathered[e, a, 2].bitcast(FP8X4), lhsT_scale=gathered[e, a, 0],
                rhs=w1[e].bitcast(FP8X4),
                rhs_scale=s1[SCALE_ROWS * (e % PLANES) : P, e // PLANES * H : (e // PLANES + 1) * H],
                start=True, stop=False,
            )

        def partner_product(e, a):
            nc.tensor.matmul_mx(
                out=first[e, a][:], lhsT=gathered[e, a, 3].bitcast(FP8X4), lhsT_scale=gathered[e, a, 1],
                rhs=wp[e].bitcast(FP4X4), rhs_scale=sp[:, e * H : (e + 1) * H], start=False, stop=True,
            )

        def first_layer(e, a, tag):
            token_product(e, a, tag)
            partner_product(e, a)

        def paired(e, a):
            return a == 0 and e < PAIRED_EXPERTS

        def rectify(e, a, engine=None, tag=None):
            relu[e, a] = sbuf([P, H], F32, f"relu{e}_{a}", tag or f"relu{e}_{a}")
            if paired(e, a):
                dst = relu[e, a][:].rearrange("s (u p d) -> s u p d", u=2, d=2)
                src = first[e, a][:].rearrange("s (p u d) -> s u p d", u=2, d=2)
            else:
                dst = relu[e, a][:].rearrange("s (t p) -> s t p", t=PACK)
                src = first[e, a][:].rearrange("s (p t) -> s t p", t=PACK)
            if engine == V:
                nc.vector.tensor_scalar(dst, src, 0.0, None, MAX)
            else:
                nc.scalar.activation(dst, src, ACT.Relu)

        def square_pairs(e):
            squared[e] = sbuf([P, H], BF16, f"squared{e}", f"hidden{e - 2}_0" if e >= 2 else f"squared{e}")
            nc.gpsimd.tensor_tensor(squared[e][:], relu[e, 0][:], relu[e, 0][:], MULT)

        def hidden_tile(e, a):
            if a == 1 and e < LAID_EXPERTS:
                hidden[e, a] = laid_tile([P, P * PACK], BF16, f"hidden{e}_{a}", e * LAID_BYTES)
            else:
                hidden[e, a] = sbuf([P, P * PACK], BF16, f"hidden{e}_{a}", f"hidden{e}_{a}")
            return hidden[e, a][:]

        def turn_pairs(e, tag):
            turned[e, 0] = bank([P, 2, P], f"turned{e}_0", tag)
            pairs = squared[e][:].bitcast(F32)
            for u in range(2):
                nc.tensor.transpose(turned[e, 0][:, u, :], pairs[:, u * P : (u + 1) * P], ident[:])

        def copy_pairs(e, copy):
            dst = hidden_tile(e, 0).bitcast(F32).rearrange("p (s u) -> p s u", u=2)
            copy(dst, turned[e, 0][:].rearrange("p u s -> p s u"))

        def turn_values(e, a, tag):
            turned[e, a] = bank([P, PACK, P], f"turned{e}_{a}", tag)
            for t in range(PACK):
                nc.tensor.transpose(turned[e, a][:, t, :], relu[e, a][:, t * P : (t + 1) * P], ident[:])

        def square_values(e, a):
            dst = hidden_tile(e, a).rearrange("p (s t) -> p s t", t=PACK)
            nc.scalar.activation(dst, turned[e, a][:].rearrange("p t s -> p s t"), ACT.Square)

        def new_codes(e):
            codes[e] = held.tile([P, C], U32, name=f"codes{e}", align_bytes=64)
            cscales[e] = held.tile([P, C], U8, name=f"cscales{e}", align_bytes=64)

        def quantize_half(e, a):
            cols = slice(a * P, (a + 1) * P)
            nc.vector.quantize_mx(out=codes[e][:, cols].bitcast(FP8X4), scales=cscales[e][:, cols], in_=hidden[e, a][:])

        def quantize(e):
            new_codes(e)
            for a in (1, 0):
                quantize_half(e, a)

        def output_block(result, e, block, slots):
            n0 = block * P
            col = e // PLANES * N + n0
            nc.tensor.matmul_mx(
                out=result, lhsT=w2[e][:, PACK * n0 : PACK * (n0 + P)].bitcast(FP8X4),
                lhsT_scale=s2[SCALE_ROWS * (e % PLANES) : P, col : col + P],
                rhs=codes[e][:, slots].bitcast(FP8X4), rhs_scale=cscales[e][:, slots], start=True, stop=True,
            )

        def finish_block(e, block, tag, copy):
            result = bank([P, C], f"result{e}_block{block}", tag)
            output_block(result[:], e, block, slice(0, C))
            tile = held.tile([P, C], F32, name=f"staged{e}_block{block}", align_bytes=64)
            copy(tile[:], result[:])
            nc.sync.dma_start(out[block * P : (block + 1) * P, e * C : (e + 1) * C], tile[:])

        def second_layer(e, part, tag):
            result = bank([P, 2, C], f"result{e}_{part}", tag)
            for j in range(2):
                output_block(result[:, j, :], e, 2 * part + j, slice(0, C))
            return result

        def store(e, part, result, copy, tag=None):
            width = 2 if e < PAIRED_STORES else 1
            first_e = e - e % width
            if (first_e, part) not in staged:
                staged[first_e, part] = sbuf([P, 2, width * C], F32, f"staged{e}_{part}", tag or f"staged{e}_{part}")
            tile = staged[first_e, part]
            copy(tile[:, :, (e - first_e) * C : (e - first_e + 1) * C], result[:])
            if e == first_e + width - 1:
                rows = out[2 * part * P : (2 * part + 2) * P, first_e * C : (e + 1) * C]
                nc.sync.dma_start(rows.rearrange("(j p) c -> p j c", p=P), tile[:])

        staged = {}
        gather_words(0, "words0")
        nc.vector.tensor_copy(x_s[:].bitcast(I32), x_s_landing[:].bitcast(I32))
        early_words = sbuf([P, 6, C], U32, "early_words", "start")
        for e in range(3):
            gather_bytes(e, f"bytes{e}")
            gather(e + 1, 1, early_words[:, 2 * e : 2 * e + 2, :])
        for e in range(E - 2):
            k = e - 2
            for a in range(HALVES):
                first_layer(e, a, f"result1_{a}" if e == 0 else f"first{a}")
                rectify(e, a)
            if k >= 0:
                quantize(k)
                gather(k + 3, 0, laid_tile([P, 2, C], U8, f"bytes{k + 3}", k * LAID_BYTES))
                gather(k + 4, 1, laid_tile([P, 2, C], U32, f"words{k + 4}", k * LAID_BYTES + 2 * C))
            square_pairs(e)
            if e >= 1:
                turn_values(e - 1, 1, "turned1")
                turn_pairs(e - 1, "turned0")
                square_values(e - 1, 1)
                copy_pairs(e - 1, nc.scalar.copy)
            if k >= 0:
                banks = [second_layer(k, part, f"result{k % 2}_{part}") for part in range(2)]
                for part in range(2):
                    store(k, part, banks[part], nc.scalar.copy)

        def finish(e, part, tag, copy):
            store(e, part, second_layer(e, part, tag), copy)

        on_scalar, on_vector = nc.scalar.copy, nc.vector.tensor_copy
        last = E - 1
        for a in range(HALVES):
            first_layer(last - 1, a, f"first{a}")
            rectify(last - 1, a)
        quantize(last - 3)
        gather_bytes(last, f"hidden{last - 3}_1")
        square_pairs(last - 1)
        turn_values(last - 2, 1, "turned1")
        turn_pairs(last - 2, "turned0")
        square_values(last - 2, 1)
        copy_pairs(last - 2, on_scalar)
        banks = [second_layer(last - 3, part, f"result0_{part}") for part in range(2)]
        for a in range(HALVES):
            token_product(last, a, f"result1_{a}")
        for a in range(HALVES):
            partner_product(last, a)
        store(last - 3, 0, banks[0], on_vector)
        store(last - 3, 1, banks[1], on_scalar)
        turn_values(last - 1, 1, "turned1")
        turn_pairs(last - 1, "turned0")
        quantize(last - 2)
        rectify(last, 0, V, f"hidden{last - 2}_1")
        rectify(last, 1, S)
        banks = [second_layer(last - 2, part, f"result0_{part}") for part in range(2)]
        for a in range(HALVES):
            turn_values(last, a, f"first{a}")
        square_values(last - 1, 1)
        copy_pairs(last - 1, on_vector)
        quantize(last - 1)
        store(last - 2, 0, banks[0], on_scalar)
        store(last - 2, 1, banks[1], on_vector, f"hidden{last - 1}_1")
        banks = [second_layer(last - 1, part, f"result1_{part}") for part in range(2)]
        for a in range(HALVES):
            square_values(last, a)
        store(last - 1, 0, banks[0], on_vector)
        quantize(last)
        store(last - 1, 1, banks[1], on_scalar)
        for block, tag in enumerate(("turned0", "turned1", "result0_0", "result0_1")):
            finish_block(last, block, tag, on_scalar if block % 2 else on_vector)
